import numpy as np, ml_dtypes
CORES = [5,29,101,125,133,157,229,253]
N = 8
BF = ml_dtypes.bfloat16
def gentries(a):
    return np.ascontiguousarray(a.reshape(8, 16, -1).transpose(0, 2, 1)).reshape(8, -1)
def gtable(e):
    e = np.asarray(e); return np.ascontiguousarray(e.reshape(8, -1, 16).transpose(0, 2, 1)).reshape(128, -1).astype(np.int32)
P, A, M, Q = 16384, 8, 8, 256
S = N * P
def letters(rng, w, n):
    a = np.add.accumulate(w); return np.searchsorted(a[:-1], rng.random(n) * a[-1], side="right")
def places(rng):
    p = rng.integers(0, S + 1, (N, 8, 2, Q)); u = P // 8
    v = rng.integers(0, 8 * N + 1, p.shape) * u + rng.integers(-1, 2, p.shape)
    p = np.sort(np.where(rng.random(p.shape) < 0.25, np.minimum(np.maximum(v, 0), S), p), axis=2)
    k = (8 * np.arange(N)[:, None] + np.arange(8)) * u
    p[:, :, 0, Q - 5] = k; p[:, :, 1, Q - 5] = k + u; p[:, :, :, Q - 4] = S; p[:, :, :, Q - 3] = 0
    p[:, :, 1, Q - 2] = p[:, :, 0, Q - 2]; p[:, :, 0, Q - 1] = 0; p[:, :, 1, Q - 1] = S
    return p
def pack(s, e, p):
    return {"bwt": np.ascontiguousarray(np.asarray(s).reshape(8, N, P).transpose(1, 0, 2)).astype(np.int32), "pats": np.stack([gtable(e[r].reshape(8, M * Q)) for r in range(N)]), "starts": np.stack([gtable(p[r].reshape(8, 2 * Q)) for r in range(N)])}
def bw(t):
    n = len(t); key = np.zeros(n, np.int64); k = 62 // (A - 1).bit_length()
    for i in range(k): key = key * A + np.roll(t, -i)
    while True:
        o = np.argsort(key); ks = key[o]
        v = np.zeros(n, np.int64); v[o[1:]] = np.add.accumulate((ks[1:] != ks[:-1]).astype(np.int64))
        if v.max() == n - 1 or k >= n: break
        key = (v * n + np.roll(v, -k)) * n + np.roll(v, -2 * k); k *= 3
    return t[o - 1]
def setup_inputs(rng):
    s = []; e = rng.integers(0, A, (N, 8, M, Q)); h = Q // 2
    for g in range(8):
        w = np.exp2(rng.integers(0, 4, A)); c = rng.integers(0, A); w[c] += 4 * A
        s.append(np.concatenate([letters(rng, w * np.exp2(rng.integers(0, 3, A)), P) for r in range(N)]))
        e[:, g, :, :h] = np.where(rng.random((N, M, h)) < 0.875, c, e[:, g, :, :h])
    return pack(np.stack(s), e, places(rng))
def setup_inputs_ends(rng):
    i = np.arange(S); s = np.zeros((8, S), np.int64)
    s[0] = i * A // S; s[1] = A - 1 - s[0]; s[2] = i % A; s[3] = rng.integers(0, A - 1, S); s[4] = rng.integers(1, A, S); s[5] = i // P % A
    s[6] = np.where((i % P == 0) | (i % P == P - 1), A - 1, rng.integers(0, A - 1, S)); s[7] = np.where(i == S - 1, A - 1, rng.integers(0, A - 1, S))
    e = rng.integers(0, A, (N, 8, M, Q)); e[..., 0] = 0; e[..., 1] = A - 1; e[..., 2] = 0; e[:, :, 0, 2] = A - 1; e[..., 3] = 0; e[:, :, M - 1, 3] = A - 1
    q = rng.integers(0, N); e[q] = rng.integers(0, A, (8, M, 1)); e[q, 0] = e[q, 0, 0, 0]
    p = places(rng); p[:, :, 0, :4] = 0; p[:, :, 1, :4] = S; p[q, :, 0] = 0; p[q, :, 1] = S
    return pack(s, e, p)
def setup_inputs_one(rng):
    k = (np.arange(8) + rng.integers(0, A)) % A; c = k[None, :, None, None]
    e = np.where(rng.random((N, 8, 1, Q)) < 0.5, c, rng.integers(0, A, (N, 8, M, Q))); e[..., 0] = k[None, :, None]
    return pack(np.repeat(k[:, None], S, axis=1), e, places(rng))
def setup_inputs_text(rng):
    s = []; e = np.zeros((N, 8, M, Q), np.int64); h = Q // 2
    for g in range(8):
        t = np.tile(letters(rng, np.exp2(rng.integers(0, 3, A)), S // 8), 8); t = np.where(rng.random(S) < 0.03125, rng.integers(0, A, S), t); s.append(bw(t))
        e[:, g] = t[(rng.integers(0, S, (N, 1, Q)) + (M - 1 - np.arange(M))[None, :, None]) % S]
    e[..., h:] = np.where(rng.random((N, 8, M, Q - h)) < 0.0625, rng.integers(0, A, (N, 8, M, Q - h)), e[..., h:])
    p = places(rng); p[:, :, 0, :h] = 0; p[:, :, 1, :h] = S
    return pack(np.stack(s), e, p)
def setup_inputs_spread(rng):
    s = np.stack([np.concatenate([letters(rng, np.exp2(-2.0 * rng.permutation(A)), P) for r in range(N)]) for g in range(8)])
    e = np.stack([s[g][rng.integers(0, S, (N, M, Q))] for g in range(8)], axis=1)
    p = places(rng); p[:, :, 1] = np.minimum(p[:, :, 0] + (rng.integers(0, S + 1, (N, 8, Q)) >> rng.integers(0, 20, (N, 8, Q))), S)
    return pack(s, np.where(rng.random((N, 8, 1, Q)) < 0.5, e, rng.integers(0, A, (N, 8, M, Q))), p)
def check_inputs(d):
    bad = [k + " out of range" for k in ("bwt", "pats") if not ((d[k] >= 0) & (d[k] < A)).all()]
    if not ((d["starts"] >= 0) & (d["starts"] <= S)).all(): bad.append("starts out of range")
    p = np.stack([gentries(a) for a in d["starts"]]).reshape(N, 8, 2, Q)
    if (p[:, :, 0] > p[:, :, 1]).any(): bad.append("lo over hi in starts")
    return bad
def reference(bwt, pats, starts):
    s = bwt.transpose(1, 0, 2).reshape(8, S)
    e = np.stack([gentries(pats[r]) for r in range(N)]).reshape(N, 8, M, Q)
    b = np.stack([gentries(starts[r]) for r in range(N)]).reshape(N, 8, 2, Q).astype(np.int64)
    ends = np.zeros((N, 8, 2, Q), np.int64)
    for g in range(8):
        C = np.array([np.count_nonzero(s[g] < c) for c in range(A)]); occ = np.zeros((A, S + 1), np.int64)
        for c in range(A): occ[c, 1:] = np.add.accumulate((s[g] == c).astype(np.int64))
        p = b[:, g]
        for t in range(M):
            c = e[:, g, t][:, None]; p = C[c] + occ[c, p]
        ends[:, g] = p
    return {"y": np.asarray(np.stack([gtable(ends[r].reshape(8, 2 * Q)) for r in range(N)]), np.float32)}

@@ -1,0 +1,379 @@
+import math
+from concourse.bass import DstId, RemoteDMATransfer
+from concourse.mybir import dt, AluOpType, AxisListType, ActivationFunctionType
+
+ALU = AluOpType
+ACT = ActivationFunctionType
+NB = 8192
+NDMA = 3
+
+
+def _sb(dtype, **kw):
+    return {n: ("sbuf", [128] + (list(w) if isinstance(w, tuple) else [w]), dtype) for n, w in kw.items()}
+
+
+SCRATCH = {"sendP": ("dram", [1024, 20], "int32"), "sendL": ("dram", [1024, 128], "bfloat16"),
+           "landP": ("dram", [1024, 20], "int32"), "landL": ("dram", [1024, 128], "bfloat16"),
+           "relP": ("dram", [128, 20], "int32"), "relL": ("dram", [128, 128], "bfloat16"),
+           "pA": ("psum", [128, 1024], "bfloat16"), "pB": ("psum", [128, 1024], "bfloat16")}
+SCRATCH.update({"p%d" % _k: ("psum", [128, 512], "float32") for _k in range(6)})
+SCRATCH.update(_sb("int32", X=(8, 8, 16), wi=128, cntI=512, PS=160, PSl=160, ip=1, irow=128, ci=8, ir16=128, irc=128, irr=128,
+                   qi0=16, qi1=16, rr0=16, rr1=16))
+SCRATCH.update(_sb("uint16", CWu=256, la0=16, la1=16, lb0=16, lb1=16))
+SCRATCH.update(_sb("float32", landR=256, w8=32, base=516, zf=512, et=16, e1=1, Res=32, cf=8, irf=128, mt=128, c99=128, tb=128,
+                   rm=8, m16=16, relR=32, W0=32, W1=32))
+SCRATCH.update(_sb("bfloat16", Xb=(8, 128), Ls=1024, clo=1024, chi=1024, cntB=512, landC=512, cur=256, cO=288, CM=2048, HL=1024,
+                   S2=1024, ehl=16, T1=NB + 16, T2=NB + 16, TB=128, TC=8, ones=128, Ib=128, Ih=128, nI=128, R1=128, Tri=128, Ind1=8,
+                   Ind8=8, Sel=1024, relC=64, G0=256, G1=256, E0=256, E1=256, F0=256, F1=256))
+
+SEMAPHORES = (["io", "c1", "c2", "c3", "c4", "c5", "c6", "c7", "on", "ms", "xb", "tA", "tB", "ev", "es", "ex0", "ex1", "pc",
+               "wi", "dg", "cb", "cbo", "ps", "sp", "stL", "own", "psl", "cu", "chp", "chv", "cw", "w8", "wini", "cm",
+               "tot", "tri", "sc", "hb", "hb2", "ml", "lo", "tS", "tS2", "s2v", "s2s", "t2", "t1", "t1s", "eh", "el", "et", "e1",
+               "end", "rs", "yo", "ys", "lsP", "lsL", "lsC", "lsR", "aP", "aC", "aRn", "aRf", "hP", "hL", "hC", "hR", "hl"]
+              + ["ld%d" % k for k in range(4)] + ["aL%d" % k for k in range(8)]
+              + ["rp%d" % k for k in range(4)] + ["rb%d" % k for k in range(4)]
+              + ["%s%d" % (n, h) for n in ("vT", "vC", "vL", "vA", "vU", "sG", "vF", "vE", "pO") for h in range(2)])
+
+
+def routes(c, T, topo):
+    near = [d for d in T.cores if d != c and topo.may_write(c, d)]
+    far = [d for d in T.cores if d != c and not topo.may_write(c, d)]
+    via = []
+    for k, d in enumerate(far):
+        hs = [h for h in topo.cores_of(c) if h != c and topo.may_write(h, d)]
+        via.append((d, hs[k % len(hs)]))
+    return near, via
+
+
+def hand_on(g, core, T, topo):
+    for c in T.cores:
+        if core not in topo.cores_of(c):
+            continue
+        for d, h in routes(c, T, topo)[1]:
+            if h != core:
+                continue
+            r = T.rank_of(c)
+            rid, pid = topo.addr(d, core)
+            m = topo.mask(core, d)
+            n = len(topo.engines(core, d))
+            jobs = [("hP", T.relP[:], T.landP[r * 128:(r + 1) * 128, :], "aP"),
+                    ("hL", T.relL[:], T.landL[r * 128:(r + 1) * 128, :], "aL%d" % r),
+                    ("hC", T.relC[:], T.landC[:, r * 64:(r + 1) * 64], "aC"),
+                    ("hR", T.relR[:], T.landR[:, r * 32:(r + 1) * 32], "aRf")]
+            for hs, src, dst, a in jobs:
+                g.wait_ge(T.sem[hs], 2)
+                g.remote_dma(out_ap=dst, in_ap=src, remote_sem=T.sem[a], local_sem=T.sem.hl, pid=pid, routing_id=rid, dma_engine_mask=m)
+            g.wait_ge(T.sem.hl, n * len(jobs))
+
+
+def rank_program(g, core, T, topo):
+    me = T.rank_of(core)
+    if me is None:
+        hand_on(g, core, T, topo)
+        return
+    v, s, pe, sy = g.vector, g.scalar, g.tensor, g.sync
+    near, via = routes(core, T, topo)
+    nearr = [T.rank_of(d) for d in near]
+    farr = [T.rank_of(d) for d, h in via]
+    nfar = {T.rank_of(c): len(topo.engines(h, core)) for c in T.cores if c != core for d, h in routes(c, T, topo)[1] if d == core}
+    off = topo.engines(core, near[0])
+    onc = [e for e in topo.engines(core, via[0][1]) if e not in off]
+    cnt, seen = {}, {}
+
+    def inc(ins, name, n=1):
+        ins.then_inc(T.sem[name], n)
+        cnt[name] = cnt.get(name, 0) + n
+
+    def wait(q, *names):
+        for name in names:
+            q.wait_ge(T.sem[name], cnt[name])
+            seen[name] = max(seen.get(name, 0), cnt[name])
+
+    def spread(srcs, dst, rel, arr, hsem, lsem):
+        tr = []
+        for k, (d, to, e, a, out) in enumerate([(d, d, off[2 * k:], arr, dst) for k, d in enumerate(near)]
+                                               + [(d, h, onc[2 * k:], hsem, rel) for k, (d, h) in enumerate(via)]):
+            rid, pid = topo.addr(to, core)
+            tr.append(RemoteDMATransfer(dst_ids=[DstId(rid=rid, pnc=pid)], dma_engine_mask=(1 << e[0]) | (1 << e[1]),
+                                        remote_sem=T.sem[a], src=srcs(T.rank_of(d)), dst=out))
+        g.remote_dma_fused(tr, local_sem=T.sem[lsem])
+        cnt[lsem] = 2 * len(tr)
+
+    cnt["aP"] = cnt["aC"] = 2 * len(near) + sum(nfar.values())
+    cnt["aRn"] = 2 * len(near)
+    cnt["aRf"] = sum(nfar.values())
+    for r in nearr:
+        cnt["aL%d" % r] = 2
+    for r in farr:
+        cnt["aL%d" % r] = nfar[r]
+
+    inc(g.iota(T.ip[:], [[0, 1]], 0, 1), "io")
+    inc(g.iota(T.irow[:], [[1, 128]], 0, 0), "io")
+    for q in range(8):
+        inc((sy if q % 2 == 0 else s).dma_start(T.X[:, q], T.bwt[q]), "ld%d" % (q // 2), 16)
+    inc(s.dma_start(T.PS[:, 0:128], T.pats[:]), "ps", 16)
+    inc(s.dma_start(T.PS[:, 128:160], T.starts[:]), "ps", 16)
+    wait(v, "io")
+    inc(v.tensor_scalar(T.ci[:, 0:1], T.ip[:], 15, None, ALU.bitwise_and), "c1")
+    inc(v.tensor_scalar(T.ci[:, 1:2], T.ip[:], 4, None, ALU.arith_shift_right), "c1")
+    inc(v.tensor_scalar(T.ci[:, 2:3], T.ip[:], 7, None, ALU.bitwise_and), "c1")
+    inc(v.tensor_scalar(T.ci[:, 3:4], T.ip[:], 3, None, ALU.arith_shift_right), "c1")
+    inc(v.tensor_copy(T.cf[:, 4:5], T.ip[:]), "c1")
+    inc(v.tensor_copy(T.irf[:], T.irow[:]), "c1")
+    wait(v, "c1")
+    inc(v.tensor_copy(T.cf[:, 0:4], T.ci[:, 0:4]), "c2")
+    inc(v.tensor_scalar(T.Ib[:], T.irow[:], T.cf[:, 4:5], None, ALU.is_equal), "c2")
+    wait(v, "c2")
+    inc(v.tensor_scalar(T.Ind1[:], T.irow[:, 0:8], T.cf[:, 1:2], None, ALU.is_equal), "c3")
+    inc(v.tensor_scalar(T.cf[:, 5:6], T.cf[:, 0:1], 8.0, T.cf[:, 1:2], ALU.mult, ALU.add), "c3")
+    wait(s, "c1")
+    inc(s.activation(T.ones[:], T.irf[:], ACT.Exp, scale=0.0), "on")
+    wait(s, "ps")
+    inc(s.dma_start(T.sendP[:], T.PS[:]), "sp", 16)
+    inc(s.dma_start(T.landP[me * 128:(me + 1) * 128, :], T.PS[16 * me:16 * me + 16, :]), "sp", 16)
+    wait(g, "sp")
+    spread(lambda r: T.sendP[r * 128:(r + 1) * 128, :], T.landP[me * 128:(me + 1) * 128, :], T.relP[:], "aP", "hP", "lsP")
+
+    for q in range(8):
+        if q % 2 == 0:
+            wait(v, "ld%d" % (q // 2))
+        inc(v.tensor_copy(T.Xb[:, :, 16 * q:16 * q + 16], T.X[:, q]), "xb")
+    wait(pe, "xb", "c2")
+    for u in range(8):
+        inc(pe.transpose((T.pA if u < 4 else T.pB)[:, u % 4 * 128:u % 4 * 128 + 128], T.Xb[:, u, :], T.Ib[:]), "tA" if u < 4 else "tB")
+    wait(v, "tA")
+    wait(s, "tB")
+    for u in range(4):
+        inc(v.tensor_copy(T.Ls[:, u::8], T.pA[:, u * 128:u * 128 + 128]), "ev")
+        inc(s.activation(T.Ls[:, u + 4::8], T.pB[:, u * 128:u * 128 + 128], ACT.Copy), "es")
+    wait(sy, "ev", "es")
+    inc(sy.dma_start(T.sendL[:], T.Ls[:]), "stL", 16)
+    for G in range(8):
+        inc(sy.dma_start(T.T1[16 * G:16 * G + 16, me * 1024:(me + 1) * 1024], T.Ls[16 * me:16 * me + 16, :]), "own", 16)
+    wait(g, "stL")
+    spread(lambda r: T.sendL[r * 128:(r + 1) * 128, :], T.landL[me * 128:(me + 1) * 128, :], T.relL[:], "aL%d" % me, "hL", "lsL")
+
+    wait(s, "ev", "es")
+    k32 = math.log(32.0)
+    for h in range(2):
+        a, b = 512 * h, 512 * h + 512
+        inc(s.activation(T.clo[:, a:b], T.Ls[:, a:b], ACT.Exp, bias=3 * k32, scale=-k32), "ex%d" % h)
+        inc(s.activation(T.chi[:, a:b], T.Ls[:, a:b], ACT.Exp, bias=-4 * k32, scale=k32), "ex%d" % h)
+    wait(pe, "c3")
+    for h in range(2):
+        wait(pe, "ex%d" % h)
+        for w, code in enumerate((T.clo, T.chi)):
+            for j in range(4 * h, 4 * h + 4):
+                inc(pe.matmul(T.p0[:, w * 64 + j:w * 64 + 64:8], code[:, j * 128:j * 128 + 128], T.Ind1[:], True, True), "pc")
+    wait(v, "c3")
+    inc(v.tensor_scalar(T.ir16[:], T.irow[:], 15, None, ALU.bitwise_and), "c4")
+    inc(v.tensor_scalar(T.irc[:], T.irow[:], 7, None, ALU.bitwise_and), "c4")
+    inc(v.tensor_scalar(T.irr[:], T.irow[:], 3, None, ALU.arith_shift_right), "c4")
+    inc(v.tensor_scalar(T.R1[:], T.irow[:], T.cf[:, 5:6], None, ALU.is_equal), "c4")
+    inc(v.tensor_scalar(T.Tri[:], T.irow[:], T.cf[:, 4:5], None, ALU.is_gt), "c4")
+    inc(v.tensor_scalar(T.nI[:], T.irow[:], T.cf[:, 4:5], -1.0, ALU.is_equal, ALU.mult), "c4")
+    inc(v.tensor_scalar(T.Ih[:], T.irow[:], T.cf[:, 4:5], 0.5, ALU.is_equal, ALU.mult), "c4")
+    inc(v.tensor_scalar(T.Ind8[:], T.irow[:, 0:8], T.cf[:, 1:2], 8.0, ALU.is_equal, ALU.mult), "c4")
+    inc(v.tensor_scalar(T.TC[:], T.irow[:, 0:8], T.cf[:, 2:3], None, ALU.is_equal), "c4")
+    inc(v.tensor_scalar(T.rm[:], T.irow[:, 0:8], T.cf[:, 2:3], None, ALU.is_equal), "c4")
+    inc(v.tensor_scalar(T.m16[:], T.irow[:, 0:16], T.cf[:, 0:1], None, ALU.is_equal), "c4")
+    inc(v.memset(T.cur[:], 0.0), "ms")
+    wait(v, "c4")
+    inc(v.tensor_scalar(T.mt[:], T.irr[:], T.cf[:, 0:1], None, ALU.is_gt), "c5")
+    inc(v.tensor_scalar(T.c99[:], T.irc[:], -99.0, None, ALU.add), "c5")
+    wait(v, "pc")
+    inc(v.tensor_scalar(T.wi[:], T.p0[:, 0:128], -0.25, None, ALU.add), "wi")
+    wait(v, "wi")
+    for j in range(4):
+        inc(v.tensor_scalar(T.cntI[:, 3 - j::8], T.wi[:, 0:64], 5 * j, 31, ALU.arith_shift_right, ALU.bitwise_and), "dg")
+        inc(v.tensor_scalar(T.cntI[:, 4 + j::8], T.wi[:, 64:128], 5 * j, 31, ALU.arith_shift_right, ALU.bitwise_and), "dg")
+    wait(v, "dg")
+    inc(v.tensor_copy(T.cntB[:], T.cntI[:]), "cb")
+    inc(v.tensor_copy(T.landC[:, me * 64:me * 64 + 64], T.cntI[:, me * 64:me * 64 + 64]), "cbo")
+    wait(g, "cb")
+    spread(lambda r: T.cntB[:, r * 64:r * 64 + 64], T.landC[:, me * 64:me * 64 + 64], T.relC[:], "aC", "hC", "lsC")
+    wait(v, "c5")
+    inc(v.tensor_tensor(T.tb[:], T.mt[:], T.c99[:], ALU.mult), "c6")
+    for r in range(NDMA, 8):
+        inc(v.tensor_scalar(T.Sel[:, r * 128:r * 128 + 128], T.ir16[:], T.cf[:, 3:4], T.rm[:, r:r + 1], ALU.is_equal, ALU.mult), "c7")
+    inc(v.memset(T.zf[:], 0.0), "ms")
+    inc(v.memset(T.base[:, 0:1], 0.0), "ms")
+    inc(v.memset(T.cO[:, 256:288], 0.0), "ms")
+    inc(v.memset(T.T1[:, NB:NB + 16], 0.0), "ms")
+    wait(v, "c6")
+    inc(v.tensor_scalar(T.TB[:], T.tb[:], 99.0, None, ALU.add), "c7")
+
+    wait(sy, "aP", "sp")
+    inc(sy.dma_start(T.PSl[:], T.landP[:]), "psl", 16)
+    wait(v, "psl", "ms")
+    for t in range(8):
+        inc(v.tensor_copy(T.cur[:, 32 * t:32 * t + 16], T.PSl[:, 16 * t:16 * t + 16]), "cu")
+    inc(v.tensor_scalar(T.w8[:], T.PSl[:, 128:160], 8.0, None, ALU.mult), "w8")
+    wait(pe, "cu", "c4")
+    for t in range(1, 8):
+        n = 256 - 32 * t
+        if t > 1:
+            wait(pe, "chv")
+        inc(pe.matmul(T.p1[:, 0:n], T.R1[:], T.cur[:, 32 * t:256], True, True), "chp")
+        wait(v, "chp")
+        inc(v.tensor_copy(T.cur[:, 32 * t:256], T.p1[:, 0:n]), "chv")
+    wait(v, "chv", "w8")
+    inc(v.tensor_copy(T.CWu[:], T.cur[:]), "cw")
+    inc(v.transpose(T.cO[:, 0:256], T.cur[:]), "cw")
+    for h in range(2):
+        inc(v.tensor_tensor(T["W%d" % h][:, 0:16], T.w8[:, 16 * h:16 * h + 16], T.cur[:, 0:16], ALU.add), "wini")
+    wait(s, "cw", "c4")
+    for t in range(8):
+        inc(s.activation(T.CM[:, 256 * t:256 * t + 256], T.TC[:, 0:8].indirect(T.CWu[:, 32 * t:32 * t + 16]), ACT.Copy), "cm")
+
+    def t1(q, r, sem):
+        wait(q, "aL%d" % r)
+        for G in range(8):
+            inc(q.dma_start(T.T1[16 * G:16 * G + 16, r * 1024:(r + 1) * 1024], T.landL[r * 128:(r + 1) * 128, :]), sem, 16)
+    for r in nearr + farr[2:]:
+        t1(sy, r, "t1")
+    for r in farr[:2]:
+        t1(s, r, "t1s")
+
+    wait(pe, "aC", "cbo", "on")
+    for c in range(8):
+        inc(pe.matmul(T.p3[:, c * 64:c * 64 + 64], T.ones[:], T.landC[:, c::8], True, True), "tot")
+    inc(pe.matmul(T.p2[:], T.Tri[:], T.landC[:], True, True), "tri")
+    wait(v, "tot")
+    inc(v.tensor_tensor_scan(T.base[:, 1:513], T.p3[:], T.zf[:], 0.0, ALU.add, ALU.add), "sc")
+    wait(v, "sc", "tri")
+    for c in range(8):
+        inc(v.tensor_tensor(T.HL[:, c * 64:c * 64 + 64], T.p2[:, c::8], T.base[:, c * 64:c * 64 + 64], ALU.add), "hb" if c < 4 else "hb2")
+    inc(v.tensor_copy(T.ehl[:, 0:8], T.base[:, 64:513:64]), "eh")
+    for c in range(8):
+        if c % 4 == 0:
+            wait(pe, "hb2" if c else "hb")
+        inc(pe.matmul(T.p4[:, c * 64:c * 64 + 64], T.Tri[:], T.landC[:, c::8], True, False), "ml")
+        inc(pe.matmul(T.p4[:, c * 64:c * 64 + 64], T.nI[:], T.HL[:, c * 64:c * 64 + 64], False, True), "ml")
+    wait(v, "eh")
+    inc(v.tensor_tensor(T.ehl[:, 8:16], T.base[:, 64:513:64], T.ehl[:, 0:8], ALU.subtract), "el")
+    wait(v, "ml")
+    inc(v.tensor_tensor(T.HL[:, 512:1024], T.p4[:], T.base[:, 0:512], ALU.add), "lo")
+    wait(v, "el")
+    inc(v.tensor_tensor(T.et[:], T.ehl[:], T.m16[:], ALU.mult), "et")
+    wait(pe, "lo", "es", "ev")
+    for j in range(8):
+        inc(pe.transpose((T.pA if j < 4 else T.pB)[:, j % 4 * 128:j % 4 * 128 + 128], T.HL[:, j::8], T.Ib[:]), "tS" if j < 4 else "tS2")
+    wait(v, "tS")
+    inc(v.tensor_copy(T.S2[:, 0:512], T.pA[:, 0:512]), "s2v")
+    wait(s, "tS2")
+    inc(s.activation(T.S2[:, 512:1024], T.pB[:, 0:512], ACT.Copy), "s2s")
+    wait(v, "et")
+    inc(v.tensor_reduce(T.e1[:], T.et[:], AxisListType.X, ALU.add), "e1")
+    wait(sy, "s2v", "s2s")
+    for r in range(NDMA):
+        for G in range(8):
+            inc(sy.dma_start(T.T2[16 * G:16 * G + 16, r * 1024:(r + 1) * 1024], T.S2[r::8, :]), "t2", 16)
+    wait(pe, "s2v", "c7")
+    i = 0
+    for hf in range(2):
+        if hf:
+            wait(pe, "s2s")
+        for r in range(NDMA, 8):
+            k = i % 4
+            if i >= 4:
+                wait(pe, "rb%d" % k)
+            inc(pe.matmul(T["p%d" % k][:], T.Sel[:, r * 128:r * 128 + 128], T.S2[:, 512 * hf:512 * hf + 512], True, True), "rp%d" % k)
+            o = T.T2[:, r * 1024 + 512 * hf:r * 1024 + 512 * hf + 512]
+            if i % 2 == 0:
+                wait(v, "rp%d" % k)
+                inc(v.tensor_copy(o, T["p%d" % k][:]), "rb%d" % k)
+            else:
+                wait(s, "rp%d" % k)
+                inc(s.activation(o, T["p%d" % k][:], ACT.Copy), "rb%d" % k)
+            i += 1
+    wait(v, "e1")
+    inc(v.tensor_copy(T.T2[:, NB:NB + 1], T.e1[:]), "end")
+
+    O = [T.p4, T.p5]
+
+    def small1(h, t):
+        W = T["W%d" % h]
+        if t > 0:
+            wait(v, "pO%d" % h)
+            inc(v.transpose(W[:, 0:32], O[h][:, 0:32]), "vT%d" % h)
+            wait(v, "vT%d" % h)
+        else:
+            wait(v, "wini")
+        if t == 8:
+            inc(v.tensor_scalar(T.Res[:, 16 * h:16 * h + 16], W[:, 0:16], 0.125, None, ALU.mult), "rs")
+            return
+        inc(v.tensor_copy(T["qi%d" % h][:], W[:, 0:16]), "vC%d" % h)
+        inc(v.tensor_scalar(T["la%d" % h][:], W[:, 0:16], 1.0 / 128, -(0.5 - 1.0 / 256), ALU.mult, ALU.add), "vL%d" % h)
+
+    def small2(h, t):
+        if t == 8:
+            return
+        wait(v, "vC%d" % h)
+        inc(v.tensor_scalar(T["rr%d" % h][:], T["qi%d" % h][:], 127, None, ALU.bitwise_and), "vA%d" % h)
+        wait(v, "vA%d" % h)
+        inc(v.tensor_copy(T["lb%d" % h][:], T["rr%d" % h][:]), "vU%d" % h)
+        wait(s, "vU%d" % h)
+        if t == 0 and h == 0:
+            wait(s, "c7")
+        inc(s.activation(T["G%d" % h][:], T.TB[:].indirect(T["lb%d" % h][:]), ACT.Copy), "sG%d" % h)
+
+    def letters(h, t, first):
+        inc(pe.matmul(O[h][:, 0:32], T.Ih[:], T.cO[:, 32 * t + 32:32 * t + 64], first, not first), "pO%d" % h)
+
+    def sums(h, X):
+        for A in range(4):
+            for ch in range(4):
+                inc(pe.matmul(O[h][32 * A:32 * A + 16, 8 * ch:8 * ch + 8], X[:, 4 * A + ch::16], T.Ind8[:], False, False), "pO%d" % h)
+
+    def occ(h, t):
+        if t == 8:
+            return
+        wait(v, "vL%d" % h)
+        if t == 0 and h == 0:
+            wait(v, "cm", "t2", "end", "rb0", "rb1", "rb2", "rb3")
+        inc(v.tensor_tensor(T["F%d" % h][:], T.T2[:, 0:NB + 1].indirect(T["la%d" % h][:]), T.CM[:, 256 * t:256 * t + 256], ALU.mult), "vF%d" % h)
+        wait(pe, "vF%d" % h)
+        if t == 0 and h == 0:
+            wait(pe, "cw", "ms")
+        letters(h, t, True)
+        sums(h, T["F%d" % h])
+
+    def fine(h, t):
+        wait(v, "sG%d" % h)
+        if t == 0 and h == 0:
+            wait(v, "own", "t1", "t1s", "ms")
+        inc(v.tensor_tensor(T["E%d" % h][:], T.T1[:, 0:NB + 1].indirect(T["la%d" % h][:]), T["G%d" % h][:], ALU.is_equal), "vE%d" % h)
+        wait(pe, "vE%d" % h)
+        sums(h, T["E%d" % h])
+        letters(h, t, False)
+
+    small1(0, 0)
+    small2(0, 0)
+    occ(0, 0)
+    small1(1, 0)
+    for t in range(8):
+        fine(0, t)
+        small2(1, t)
+        occ(1, t)
+        small1(0, t + 1)
+        fine(1, t)
+        small2(0, t + 1)
+        occ(0, t + 1)
+        small1(1, t + 1)
+
+    wait(g, "rs")
+    spread(lambda r: T.Res[:], T.landR[:, me * 32:me * 32 + 32], T.relR[:], "aRn", "hR", "lsR")
+    wait(sy, "rs")
+    inc(sy.dma_start(T.y[16 * me:16 * me + 16, :], T.Res[me::8, :]), "yo", 16)
+    wait(sy, "aRn")
+    wait(sy, "aRf")
+    wait(s, "aRf", "aRn")
+    for k, r in enumerate(nearr + farr):
+        sc = k >= 5
+        inc((s if sc else sy).dma_start(T.y[16 * r:16 * r + 16, :], T.landR[me::8, r * 32:r * 32 + 32]), "ys" if sc else "yo", 16)
+    wait(sy, "yo")
+    wait(s, "ys")
+    for name in cnt:
+        if seen.get(name, 0) < cnt[name]:
+            wait(g, name)

@@ -12,27 +12,31 @@ def _sb(dtype, **kw):
     return {n: ("sbuf", [128] + (list(w) if isinstance(w, tuple) else [w]), dtype) for n, w in kw.items()}
 
 
-SCRATCH = {"sendP": ("dram", [1024, 20], "int32"), "sendL": ("dram", [1024, 128], "bfloat16"),
-           "landP": ("dram", [1024, 20], "int32"), "landL": ("dram", [1024, 128], "bfloat16"),
-           "relP": ("dram", [128, 20], "int32"), "relL": ("dram", [128, 128], "bfloat16"),
+SCRATCH = {"sendL": ("dram", [1024, 128], "bfloat16"), "landL": ("dram", [1024, 128], "bfloat16"),
+           "relL": ("dram", [128, 128], "bfloat16"),
            "pA": ("psum", [128, 1024], "bfloat16"), "pB": ("psum", [128, 1024], "bfloat16")}
+for _n, _w in (("P", 16), ("S", 4)):
+    SCRATCH.update({"send" + _n: ("dram", [1024, _w], "int32"), "land" + _n: ("dram", [1024, _w], "int32"),
+                    "rel" + _n: ("dram", [128, _w], "int32")})
 SCRATCH.update({"p%d" % _k: ("psum", [128, 512], "float32") for _k in range(6)})
-SCRATCH.update(_sb("int32", X=(8, 8, 16), wi=128, cntI=512, PS=160, PSl=160, ip=1, irow=128, ci=8, ir16=128, irc=128, irr=128,
+SCRATCH.update(_sb("int32", X=(8, 8, 16), wi=128, cntI=512, PSl=160, ip=1, irow=128, ci=8, ir16=128, irc=128, irr=128,
                    qi0=16, qi1=16, rr0=16, rr1=16))
-SCRATCH.update(_sb("uint16", CWu=256, la0=16, la1=16, lb0=16, lb1=16))
+SCRATCH.update(_sb("uint16", CWu=128, la0=16, la1=16, lb0=16, lb1=16))
 SCRATCH.update(_sb("float32", landR=256, w8=32, base=516, zf=512, et=16, e1=1, Res=32, cf=8, irf=128, mt=128, c99=128, tb=128,
                    rm=8, m16=16, relR=32, W0=32, W1=32))
 SCRATCH.update(_sb("bfloat16", Xb=(8, 128), Ls=1024, clo=1024, chi=1024, cntB=512, landC=512, cur=256, cO=288, CM=2048, HL=1024,
-                   S2=1024, ehl=16, T1=NB + 16, T2=NB + 16, TB=128, TC=8, ones=128, Ib=128, Ih=128, nI=128, R1=128, Tri=128, Ind1=8,
-                   Ind8=8, Sel=1024, relC=64, G0=256, G1=256, E0=256, E1=256, F0=256, F1=256))
+                   S2=1024, ehl=16, T1=NB + 16, T2=NB + 16, TB=128, TC=8, ones=128, Ib=128, Ih=128, nI=128, RR=1024, Tri=128,
+                   Ind1=8, Ind8=8, Sel=1024, patb=128, relC=64, G0=256, G1=256, E0=256, E1=256, F0=256, F1=256))
 
 SEMAPHORES = (["io", "c1", "c2", "c3", "c4", "c5", "c6", "c7", "on", "ms", "xb", "tA", "tB", "ev", "es", "ex0", "ex1", "pc",
-               "wi", "dg", "cb", "cbo", "ps", "sp", "stL", "own", "psl", "cu", "chp", "chv", "cw", "w8", "wini", "cm",
-               "tot", "tri", "sc", "hb", "hb2", "ml", "lo", "tS", "tS2", "s2v", "s2s", "t2", "t1", "t1s", "eh", "el", "et", "e1",
-               "end", "rs", "yo", "ys", "lsP", "lsL", "lsC", "lsR", "aP", "aC", "aRn", "aRf", "hP", "hL", "hC", "hR", "hl"]
+               "wi", "dg", "cb", "cbo", "spP", "spS", "own2", "stL", "own", "psl", "cu", "chp", "chv", "pt", "cwu", "cwp", "cw",
+               "w8", "wini", "cm", "tot", "tri", "sc", "hb", "hb2", "ml", "lo", "tS", "tS2", "s2v", "s2s", "t2", "t1", "t1s",
+               "eh", "el", "et", "e1", "end", "rs", "yo", "ys", "lsP", "lsS", "lsL", "lsC", "lsR", "aP", "aS", "aC", "aRn", "aRf",
+               "hP", "hS", "hL", "hC", "hR", "hl"]
               + ["ld%d" % k for k in range(4)] + ["aL%d" % k for k in range(8)]
               + ["rp%d" % k for k in range(4)] + ["rb%d" % k for k in range(4)]
               + ["%s%d" % (n, h) for n in ("vT", "vC", "vL", "vA", "vU", "sG", "vF", "vE", "pO") for h in range(2)])
+WN, WF = 2, 4
 
 
 def routes(c, T, topo):
@@ -57,11 +61,12 @@ def hand_on(g, core, T, topo):
             m = topo.mask(core, d)
             n = len(topo.engines(core, d))
             jobs = [("hP", T.relP[:], T.landP[r * 128:(r + 1) * 128, :], "aP"),
+                    ("hS", T.relS[:], T.landS[r * 128:(r + 1) * 128, :], "aS"),
                     ("hL", T.relL[:], T.landL[r * 128:(r + 1) * 128, :], "aL%d" % r),
                     ("hC", T.relC[:], T.landC[:, r * 64:(r + 1) * 64], "aC"),
                     ("hR", T.relR[:], T.landR[:, r * 32:(r + 1) * 32], "aRf")]
             for hs, src, dst, a in jobs:
-                g.wait_ge(T.sem[hs], 2)
+                g.wait_ge(T.sem[hs], WF)
                 g.remote_dma(out_ap=dst, in_ap=src, remote_sem=T.sem[a], local_sem=T.sem.hl, pid=pid, routing_id=rid, dma_engine_mask=m)
             g.wait_ge(T.sem.hl, n * len(jobs))
 
@@ -77,7 +82,7 @@ def rank_program(g, core, T, topo):
     farr = [T.rank_of(d) for d, h in via]
     nfar = {T.rank_of(c): len(topo.engines(h, core)) for c in T.cores if c != core for d, h in routes(c, T, topo)[1] if d == core}
     off = topo.engines(core, near[0])
-    onc = [e for e in topo.engines(core, via[0][1]) if e not in off]
+    onc = topo.engines(core, via[0][1])
     cnt, seen = {}, {}
 
     def inc(ins, name, n=1):
@@ -89,30 +94,40 @@ def rank_program(g, core, T, topo):
             q.wait_ge(T.sem[name], cnt[name])
             seen[name] = max(seen.get(name, 0), cnt[name])
 
-    def spread(srcs, dst, rel, arr, hsem, lsem):
+    def fan(jobs, engines, w, srcs, out, sem, lsem):
         tr = []
-        for k, (d, to, e, a, out) in enumerate([(d, d, off[2 * k:], arr, dst) for k, d in enumerate(near)]
-                                               + [(d, h, onc[2 * k:], hsem, rel) for k, (d, h) in enumerate(via)]):
+        for k, (d, to) in enumerate(jobs):
             rid, pid = topo.addr(to, core)
-            tr.append(RemoteDMATransfer(dst_ids=[DstId(rid=rid, pnc=pid)], dma_engine_mask=(1 << e[0]) | (1 << e[1]),
-                                        remote_sem=T.sem[a], src=srcs(T.rank_of(d)), dst=out))
+            tr.append(RemoteDMATransfer(dst_ids=[DstId(rid=rid, pnc=pid)], dma_engine_mask=sum(1 << e for e in engines[w * k:w * k + w]),
+                                        remote_sem=T.sem[sem], src=srcs(T.rank_of(d)), dst=out))
         g.remote_dma_fused(tr, local_sem=T.sem[lsem])
-        cnt[lsem] = 2 * len(tr)
+        cnt[lsem] = cnt.get(lsem, 0) + w * len(tr)
 
-    cnt["aP"] = cnt["aC"] = 2 * len(near) + sum(nfar.values())
-    cnt["aRn"] = 2 * len(near)
+    def spread(srcs, dst, rel, arr, hsem, lsem):
+        fan(via, onc, WF, srcs, rel, hsem, lsem)
+        fan([(d, d) for d in near], off, WN, srcs, dst, arr, lsem)
+
+    cnt["aP"] = cnt["aS"] = cnt["aC"] = WN * len(near) + sum(nfar.values())
+    cnt["aRn"] = WN * len(near)
     cnt["aRf"] = sum(nfar.values())
     for r in nearr:
-        cnt["aL%d" % r] = 2
+        cnt["aL%d" % r] = WN
     for r in farr:
         cnt["aL%d" % r] = nfar[r]
+    mine = slice(me * 128, me * 128 + 128)
 
     inc(g.iota(T.ip[:], [[0, 1]], 0, 1), "io")
     inc(g.iota(T.irow[:], [[1, 128]], 0, 0), "io")
     for q in range(8):
         inc((sy if q % 2 == 0 else s).dma_start(T.X[:, q], T.bwt[q]), "ld%d" % (q // 2), 16)
-    inc(s.dma_start(T.PS[:, 0:128], T.pats[:]), "ps", 16)
-    inc(s.dma_start(T.PS[:, 128:160], T.starts[:]), "ps", 16)
+    inc(sy.dma_start(T.sendP[:], T.pats[:]), "spP", 16)
+    inc(s.dma_start(T.sendS[:], T.starts[:]), "spS", 16)
+    inc(sy.dma_start(T.landP[mine, :], T.pats[16 * me:16 * me + 16, :]), "own2", 16)
+    inc(s.dma_start(T.landS[mine, :], T.starts[16 * me:16 * me + 16, :]), "own2", 16)
+    wait(g, "spP")
+    spread(lambda r: T.sendP[r * 128:(r + 1) * 128, :], T.landP[mine, :], T.relP[:], "aP", "hP", "lsP")
+    wait(g, "spS")
+    spread(lambda r: T.sendS[r * 128:(r + 1) * 128, :], T.landS[mine, :], T.relS[:], "aS", "hS", "lsS")
     wait(v, "io")
     inc(v.tensor_scalar(T.ci[:, 0:1], T.ip[:], 15, None, ALU.bitwise_and), "c1")
     inc(v.tensor_scalar(T.ci[:, 1:2], T.ip[:], 4, None, ALU.arith_shift_right), "c1")
@@ -126,13 +141,9 @@ def rank_program(g, core, T, topo):
     wait(v, "c2")
     inc(v.tensor_scalar(T.Ind1[:], T.irow[:, 0:8], T.cf[:, 1:2], None, ALU.is_equal), "c3")
     inc(v.tensor_scalar(T.cf[:, 5:6], T.cf[:, 0:1], 8.0, T.cf[:, 1:2], ALU.mult, ALU.add), "c3")
+    inc(v.tensor_scalar(T.cf[:, 6:7], T.cf[:, 2:3], 16.0, T.cf[:, 3:4], ALU.mult, ALU.add), "c3")
     wait(s, "c1")
     inc(s.activation(T.ones[:], T.irf[:], ACT.Exp, scale=0.0), "on")
-    wait(s, "ps")
-    inc(s.dma_start(T.sendP[:], T.PS[:]), "sp", 16)
-    inc(s.dma_start(T.landP[me * 128:(me + 1) * 128, :], T.PS[16 * me:16 * me + 16, :]), "sp", 16)
-    wait(g, "sp")
-    spread(lambda r: T.sendP[r * 128:(r + 1) * 128, :], T.landP[me * 128:(me + 1) * 128, :], T.relP[:], "aP", "hP", "lsP")
 
     for q in range(8):
         if q % 2 == 0:
@@ -151,7 +162,7 @@ def rank_program(g, core, T, topo):
     for G in range(8):
         inc(sy.dma_start(T.T1[16 * G:16 * G + 16, me * 1024:(me + 1) * 1024], T.Ls[16 * me:16 * me + 16, :]), "own", 16)
     wait(g, "stL")
-    spread(lambda r: T.sendL[r * 128:(r + 1) * 128, :], T.landL[me * 128:(me + 1) * 128, :], T.relL[:], "aL%d" % me, "hL", "lsL")
+    spread(lambda r: T.sendL[r * 128:(r + 1) * 128, :], T.landL[mine, :], T.relL[:], "aL%d" % me, "hL", "lsL")
 
     wait(s, "ev", "es")
     k32 = math.log(32.0)
@@ -165,11 +176,13 @@ def rank_program(g, core, T, topo):
         for w, code in enumerate((T.clo, T.chi)):
             for j in range(4 * h, 4 * h + 4):
                 inc(pe.matmul(T.p0[:, w * 64 + j:w * 64 + 64:8], code[:, j * 128:j * 128 + 128], T.Ind1[:], True, True), "pc")
+    R = [T.Ib[:]] + [T.RR[:, t * 128:t * 128 + 128] for t in range(1, 7)] + [T.Ib[:]]
     wait(v, "c3")
     inc(v.tensor_scalar(T.ir16[:], T.irow[:], 15, None, ALU.bitwise_and), "c4")
     inc(v.tensor_scalar(T.irc[:], T.irow[:], 7, None, ALU.bitwise_and), "c4")
     inc(v.tensor_scalar(T.irr[:], T.irow[:], 3, None, ALU.arith_shift_right), "c4")
-    inc(v.tensor_scalar(T.R1[:], T.irow[:], T.cf[:, 5:6], None, ALU.is_equal), "c4")
+    inc(v.tensor_scalar(R[1], T.irow[:], T.cf[:, 5:6], None, ALU.is_equal), "c4")
+    inc(v.tensor_scalar(R[6], T.irow[:], T.cf[:, 6:7], None, ALU.is_equal), "c4")
     inc(v.tensor_scalar(T.Tri[:], T.irow[:], T.cf[:, 4:5], None, ALU.is_gt), "c4")
     inc(v.tensor_scalar(T.nI[:], T.irow[:], T.cf[:, 4:5], -1.0, ALU.is_equal, ALU.mult), "c4")
     inc(v.tensor_scalar(T.Ih[:], T.irow[:], T.cf[:, 4:5], 0.5, ALU.is_equal, ALU.mult), "c4")
@@ -177,10 +190,6 @@ def rank_program(g, core, T, topo):
     inc(v.tensor_scalar(T.TC[:], T.irow[:, 0:8], T.cf[:, 2:3], None, ALU.is_equal), "c4")
     inc(v.tensor_scalar(T.rm[:], T.irow[:, 0:8], T.cf[:, 2:3], None, ALU.is_equal), "c4")
     inc(v.tensor_scalar(T.m16[:], T.irow[:, 0:16], T.cf[:, 0:1], None, ALU.is_equal), "c4")
-    inc(v.memset(T.cur[:], 0.0), "ms")
-    wait(v, "c4")
-    inc(v.tensor_scalar(T.mt[:], T.irr[:], T.cf[:, 0:1], None, ALU.is_gt), "c5")
-    inc(v.tensor_scalar(T.c99[:], T.irc[:], -99.0, None, ALU.add), "c5")
     wait(v, "pc")
     inc(v.tensor_scalar(T.wi[:], T.p0[:, 0:128], -0.25, None, ALU.add), "wi")
     wait(v, "wi")
@@ -192,6 +201,19 @@ def rank_program(g, core, T, topo):
     inc(v.tensor_copy(T.landC[:, me * 64:me * 64 + 64], T.cntI[:, me * 64:me * 64 + 64]), "cbo")
     wait(g, "cb")
     spread(lambda r: T.cntB[:, r * 64:r * 64 + 64], T.landC[:, me * 64:me * 64 + 64], T.relC[:], "aC", "hC", "lsC")
+    wait(v, "c4")
+    inc(v.tensor_scalar(T.mt[:], T.irr[:], T.cf[:, 0:1], None, ALU.is_gt), "c5")
+    inc(v.tensor_scalar(T.c99[:], T.irc[:], -99.0, None, ALU.add), "c5")
+    inc(v.memset(T.cur[:], 0.0), "ms")
+    wait(pe, "c4")
+    for new in ([(2, 6, R[1])], [(3, 6, R[2]), (5, 2, T.Ib[:])], [(4, 6, R[3])]):
+        if new[0][0] != 2:
+            wait(pe, "chv")
+        for t, a, b in new:
+            inc(pe.matmul(T.p1[:, 128 * t - 256:128 * t - 128], R[a], b, True, True), "chp")
+        wait(v, "chp")
+        for t, a, b in new:
+            inc(v.tensor_copy(R[t], T.p1[:, 128 * t - 256:128 * t - 128]), "chv")
     wait(v, "c5")
     inc(v.tensor_tensor(T.tb[:], T.mt[:], T.c99[:], ALU.mult), "c6")
     for r in range(NDMA, 8):
@@ -203,28 +225,28 @@ def rank_program(g, core, T, topo):
     wait(v, "c6")
     inc(v.tensor_scalar(T.TB[:], T.tb[:], 99.0, None, ALU.add), "c7")
 
-    wait(sy, "aP", "sp")
-    inc(sy.dma_start(T.PSl[:], T.landP[:]), "psl", 16)
+    wait(sy, "aP", "aS", "own2")
+    inc(sy.dma_start(T.PSl[:, 0:128], T.landP[:]), "psl", 16)
+    inc(sy.dma_start(T.PSl[:, 128:160], T.landS[:]), "psl", 16)
     wait(v, "psl", "ms")
-    for t in range(8):
-        inc(v.tensor_copy(T.cur[:, 32 * t:32 * t + 16], T.PSl[:, 16 * t:16 * t + 16]), "cu")
+    inc(v.tensor_copy(T.patb[:], T.PSl[:, 0:128]), "cu")
     inc(v.tensor_scalar(T.w8[:], T.PSl[:, 128:160], 8.0, None, ALU.mult), "w8")
-    wait(pe, "cu", "c4")
-    for t in range(1, 8):
-        n = 256 - 32 * t
-        if t > 1:
-            wait(pe, "chv")
-        inc(pe.matmul(T.p1[:, 0:n], T.R1[:], T.cur[:, 32 * t:256], True, True), "chp")
-        wait(v, "chp")
-        inc(v.tensor_copy(T.cur[:, 32 * t:256], T.p1[:, 0:n]), "chv")
-    wait(v, "chv", "w8")
-    inc(v.tensor_copy(T.CWu[:], T.cur[:]), "cw")
+    wait(pe, "cu", "chv")
+    for t in range(8):
+        inc(pe.matmul(T.p0[:, 16 * t:16 * t + 16], R[t], T.patb[:, 16 * t:16 * t + 16], True, True), "pt")
+    wait(v, "pt", "w8")
+    inc(v.tensor_copy(T.CWu[:], T.p0[:, 0:128]), "cwu")
+    for t in range(8):
+        inc(v.tensor_copy(T.cur[:, 32 * t:32 * t + 16], T.p0[:, 16 * t:16 * t + 16]), "cwp")
+    wait(v, "cwp")
     inc(v.transpose(T.cO[:, 0:256], T.cur[:]), "cw")
     for h in range(2):
         inc(v.tensor_tensor(T["W%d" % h][:, 0:16], T.w8[:, 16 * h:16 * h + 16], T.cur[:, 0:16], ALU.add), "wini")
-    wait(s, "cw", "c4")
-    for t in range(8):
-        inc(s.activation(T.CM[:, 256 * t:256 * t + 256], T.TC[:, 0:8].indirect(T.CWu[:, 32 * t:32 * t + 16]), ACT.Copy), "cm")
+
+    def rows(t):
+        inc(s.activation(T.CM[:, 256 * t:256 * t + 256], T.TC[:, 0:8].indirect(T.CWu[:, 16 * t:16 * t + 16]), ACT.Copy), "cm")
+    wait(s, "cwu", "c4")
+    rows(0)
 
     def t1(q, r, sem):
         wait(q, "aL%d" % r)
@@ -317,6 +339,8 @@ def rank_program(g, core, T, topo):
         if t == 0 and h == 0:
             wait(s, "c7")
         inc(s.activation(T["G%d" % h][:], T.TB[:].indirect(T["lb%d" % h][:]), ACT.Copy), "sG%d" % h)
+        if h == 1 and t < 7:
+            rows(t + 1)
 
     def letters(h, t, first):
         inc(pe.matmul(O[h][:, 0:32], T.Ih[:], T.cO[:, 32 * t + 32:32 * t + 64], first, not first), "pO%d" % h)
@@ -330,8 +354,10 @@ def rank_program(g, core, T, topo):
         if t == 8:
             return
         wait(v, "vL%d" % h)
+        if h == 0:
+            wait(v, "cm")
         if t == 0 and h == 0:
-            wait(v, "cm", "t2", "end", "rb0", "rb1", "rb2", "rb3")
+            wait(v, "t2", "end", "rb0", "rb1", "rb2", "rb3")
         inc(v.tensor_tensor(T["F%d" % h][:], T.T2[:, 0:NB + 1].indirect(T["la%d" % h][:]), T.CM[:, 256 * t:256 * t + 256], ALU.mult), "vF%d" % h)
         wait(pe, "vF%d" % h)
         if t == 0 and h == 0:
@@ -364,14 +390,18 @@ def rank_program(g, core, T, topo):
 
     wait(g, "rs")
     spread(lambda r: T.Res[:], T.landR[:, me * 32:me * 32 + 32], T.relR[:], "aRn", "hR", "lsR")
+
+    def y(q, r, src, sem):
+        inc(q.dma_start(T.y[16 * r:16 * r + 16, :], src), sem, 16)
     wait(sy, "rs")
-    inc(sy.dma_start(T.y[16 * me:16 * me + 16, :], T.Res[me::8, :]), "yo", 16)
+    y(sy, me, T.Res[me::8, :], "yo")
     wait(sy, "aRn")
+    for r in nearr:
+        y(sy, r, T.landR[me::8, r * 32:r * 32 + 32], "yo")
     wait(sy, "aRf")
-    wait(s, "aRf", "aRn")
-    for k, r in enumerate(nearr + farr):
-        sc = k >= 5
-        inc((s if sc else sy).dma_start(T.y[16 * r:16 * r + 16, :], T.landR[me::8, r * 32:r * 32 + 32]), "ys" if sc else "yo", 16)
+    wait(s, "aRf")
+    for k, r in enumerate(farr):
+        y((sy, s)[k % 2], r, T.landR[me::8, r * 32:r * 32 + 32], ("yo", "ys")[k % 2])
     wait(sy, "yo")
     wait(s, "ys")
     for name in cnt:

@@ -21,21 +21,21 @@ for _n, _w in (("P", 16), ("S", 4)):
 SCRATCH.update({"p%d" % _k: ("psum", [128, 512], "float32") for _k in range(6)})
 SCRATCH.update(_sb("int32", X=(8, 8, 16), wi=128, cntI=512, PSl=160, ip=1, irow=128, ci=8, ir16=128, irc=128, irr=128,
                    qi0=16, qi1=16, rr0=16, rr1=16))
-SCRATCH.update(_sb("uint16", CWu=128, la0=16, la1=16, lb0=16, lb1=16))
+SCRATCH.update(_sb("uint16", CWu=128, CWo=64, la0=16, la1=16, lb0=16, lb1=16))
 SCRATCH.update(_sb("float32", landR=256, w8=32, base=516, zf=512, et=16, e1=1, Res=32, cf=8, irf=128, mt=128, c99=128, tb=128,
-                   rm=8, m16=16, relR=32, W0=32, W1=32))
-SCRATCH.update(_sb("bfloat16", Xb=(8, 128), Ls=1024, clo=1024, chi=1024, cntB=512, landC=512, cur=256, cO=288, CM=2048, HL=1024,
-                   S2=1024, ehl=16, T1=NB + 16, T2=NB + 16, TB=128, TC=8, ones=128, Ib=128, Ih=128, nI=128, RR=1024, Tri=128,
-                   Ind1=8, Ind8=8, Sel=1024, patb=128, relC=64, G0=256, G1=256, E0=256, E1=256, F0=256, F1=256))
+                   rm=8, m16=16, relR=32, W0=16, W1=16))
+SCRATCH.update(_sb("bfloat16", Xb=(8, 128), Ls=1024, clo=1024, chi=1024, cntB=512, landC=512, zc=16, cOo=64, CM=2048, HL=1024,
+                   S2=1024, ehl=16, T1=NB + 16, T2=NB + 16, TB=128, TC=8, LV=8, ones=128, Ib=128, Ih=128, Tri=128, SW=1024,
+                   Ind1=8, Ind8=8, Sel=1024, patb=128, relC=64, L0=256, L1=256, E0=256, E1=256, F0=256, F1=256))
 
-SEMAPHORES = (["io", "c1", "c2", "c3", "c4", "c5", "c6", "c7", "on", "ms", "xb", "tA", "tB", "ev", "es", "ex0", "ex1", "pc",
-               "wi", "dg", "cb", "cbo", "spP", "spS", "own2", "stL", "own", "psl", "cu", "chp", "chv", "pt", "cwu", "cwp", "cw",
-               "w8", "wini", "cm", "tot", "tri", "sc", "hb", "hb2", "ml", "lo", "tS", "tS2", "s2v", "s2s", "t2", "t1", "t1s",
-               "eh", "el", "et", "e1", "end", "rs", "yo", "ys", "lsP", "lsS", "lsL", "lsC", "lsR", "aP", "aS", "aC", "aRn", "aRf",
-               "hP", "hS", "hL", "hC", "hR", "hl"]
+SEMAPHORES = (["io", "c1", "c2", "c3", "c4", "c5", "c6", "c7", "on", "ms", "xb", "tA", "tB", "ev", "ex0", "ex1", "pc",
+               "wi", "dg", "cb", "cbn", "cbo", "spP", "spS", "own2", "stL", "own", "psl", "cu", "sw", "swp", "cwo",
+               "w8", "wini", "cm", "tot", "tri", "sc", "va0", "va1", "hi0", "hi1", "lo0", "lo1", "tS", "tS2", "s2a", "s2b", "t2",
+               "t1", "eh", "el", "et", "e1", "end", "rs", "yo", "ys", "lsP", "lsS", "lsL", "lsC", "lsR", "aP", "aS", "aC",
+               "aRn", "aRf", "hP", "hS", "hL", "hC", "hR", "hl"]
               + ["ld%d" % k for k in range(4)] + ["aL%d" % k for k in range(8)]
               + ["rp%d" % k for k in range(4)] + ["rb%d" % k for k in range(4)]
-              + ["%s%d" % (n, h) for n in ("vT", "vC", "vL", "vA", "vU", "sG", "vF", "vE", "pO") for h in range(2)])
+              + ["%s%d" % (n, h) for n in ("vC", "vL", "vA", "vU", "sG", "vF", "vE", "pO") for h in range(2)])
 WN, WF = 2, 4
 
 
@@ -103,8 +103,10 @@ def rank_program(g, core, T, topo):
         g.remote_dma_fused(tr, local_sem=T.sem[lsem])
         cnt[lsem] = cnt.get(lsem, 0) + w * len(tr)
 
-    def spread(srcs, dst, rel, arr, hsem, lsem):
+    def spread(srcs, dst, rel, arr, hsem, lsem, between=None):
         fan(via, onc, WF, srcs, rel, hsem, lsem)
+        if between:
+            wait(g, between)
         fan([(d, d) for d in near], off, WN, srcs, dst, arr, lsem)
 
     cnt["aP"] = cnt["aS"] = cnt["aC"] = WN * len(near) + sum(nfar.values())
@@ -118,10 +120,10 @@ def rank_program(g, core, T, topo):
 
     inc(g.iota(T.ip[:], [[0, 1]], 0, 1), "io")
     inc(g.iota(T.irow[:], [[1, 128]], 0, 0), "io")
-    for q in range(8):
-        inc((sy if q % 2 == 0 else s).dma_start(T.X[:, q], T.bwt[q]), "ld%d" % (q // 2), 16)
     inc(sy.dma_start(T.sendP[:], T.pats[:]), "spP", 16)
     inc(s.dma_start(T.sendS[:], T.starts[:]), "spS", 16)
+    for q in range(8):
+        inc((sy if q % 2 == 0 else s).dma_start(T.X[:, q], T.bwt[q]), "ld%d" % (q // 2), 16)
     inc(sy.dma_start(T.landP[mine, :], T.pats[16 * me:16 * me + 16, :]), "own2", 16)
     inc(s.dma_start(T.landS[mine, :], T.starts[16 * me:16 * me + 16, :]), "own2", 16)
     wait(g, "spP")
@@ -140,8 +142,6 @@ def rank_program(g, core, T, topo):
     inc(v.tensor_scalar(T.Ib[:], T.irow[:], T.cf[:, 4:5], None, ALU.is_equal), "c2")
     wait(v, "c2")
     inc(v.tensor_scalar(T.Ind1[:], T.irow[:, 0:8], T.cf[:, 1:2], None, ALU.is_equal), "c3")
-    inc(v.tensor_scalar(T.cf[:, 5:6], T.cf[:, 0:1], 8.0, T.cf[:, 1:2], ALU.mult, ALU.add), "c3")
-    inc(v.tensor_scalar(T.cf[:, 6:7], T.cf[:, 2:3], 16.0, T.cf[:, 3:4], ALU.mult, ALU.add), "c3")
     wait(s, "c1")
     inc(s.activation(T.ones[:], T.irf[:], ACT.Exp, scale=0.0), "on")
 
@@ -152,19 +152,18 @@ def rank_program(g, core, T, topo):
     wait(pe, "xb", "c2")
     for u in range(8):
         inc(pe.transpose((T.pA if u < 4 else T.pB)[:, u % 4 * 128:u % 4 * 128 + 128], T.Xb[:, u, :], T.Ib[:]), "tA" if u < 4 else "tB")
-    wait(v, "tA")
-    wait(s, "tB")
-    for u in range(4):
-        inc(v.tensor_copy(T.Ls[:, u::8], T.pA[:, u * 128:u * 128 + 128]), "ev")
-        inc(s.activation(T.Ls[:, u + 4::8], T.pB[:, u * 128:u * 128 + 128], ACT.Copy), "es")
-    wait(sy, "ev", "es")
+    for u in range(8):
+        if u % 4 == 0:
+            wait(v, "tB" if u else "tA")
+        inc(v.tensor_copy(T.Ls[:, u::8], (T.pA if u < 4 else T.pB)[:, u % 4 * 128:u % 4 * 128 + 128]), "ev")
+    wait(sy, "ev")
     inc(sy.dma_start(T.sendL[:], T.Ls[:]), "stL", 16)
     for G in range(8):
         inc(sy.dma_start(T.T1[16 * G:16 * G + 16, me * 1024:(me + 1) * 1024], T.Ls[16 * me:16 * me + 16, :]), "own", 16)
     wait(g, "stL")
     spread(lambda r: T.sendL[r * 128:(r + 1) * 128, :], T.landL[mine, :], T.relL[:], "aL%d" % me, "hL", "lsL")
 
-    wait(s, "ev", "es")
+    wait(s, "ev")
     k32 = math.log(32.0)
     for h in range(2):
         a, b = 512 * h, 512 * h + 512
@@ -176,18 +175,14 @@ def rank_program(g, core, T, topo):
         for w, code in enumerate((T.clo, T.chi)):
             for j in range(4 * h, 4 * h + 4):
                 inc(pe.matmul(T.p0[:, w * 64 + j:w * 64 + 64:8], code[:, j * 128:j * 128 + 128], T.Ind1[:], True, True), "pc")
-    R = [T.Ib[:]] + [T.RR[:, t * 128:t * 128 + 128] for t in range(1, 7)] + [T.Ib[:]]
-    wait(v, "c3")
     inc(v.tensor_scalar(T.ir16[:], T.irow[:], 15, None, ALU.bitwise_and), "c4")
     inc(v.tensor_scalar(T.irc[:], T.irow[:], 7, None, ALU.bitwise_and), "c4")
     inc(v.tensor_scalar(T.irr[:], T.irow[:], 3, None, ALU.arith_shift_right), "c4")
-    inc(v.tensor_scalar(R[1], T.irow[:], T.cf[:, 5:6], None, ALU.is_equal), "c4")
-    inc(v.tensor_scalar(R[6], T.irow[:], T.cf[:, 6:7], None, ALU.is_equal), "c4")
     inc(v.tensor_scalar(T.Tri[:], T.irow[:], T.cf[:, 4:5], None, ALU.is_gt), "c4")
-    inc(v.tensor_scalar(T.nI[:], T.irow[:], T.cf[:, 4:5], -1.0, ALU.is_equal, ALU.mult), "c4")
     inc(v.tensor_scalar(T.Ih[:], T.irow[:], T.cf[:, 4:5], 0.5, ALU.is_equal, ALU.mult), "c4")
     inc(v.tensor_scalar(T.Ind8[:], T.irow[:, 0:8], T.cf[:, 1:2], 8.0, ALU.is_equal, ALU.mult), "c4")
     inc(v.tensor_scalar(T.TC[:], T.irow[:, 0:8], T.cf[:, 2:3], None, ALU.is_equal), "c4")
+    inc(v.tensor_scalar(T.LV[:], T.irow[:, 0:8], 1.0 / 16, None, ALU.mult), "c4")
     inc(v.tensor_scalar(T.rm[:], T.irow[:, 0:8], T.cf[:, 2:3], None, ALU.is_equal), "c4")
     inc(v.tensor_scalar(T.m16[:], T.irow[:, 0:16], T.cf[:, 0:1], None, ALU.is_equal), "c4")
     wait(v, "pc")
@@ -197,31 +192,22 @@ def rank_program(g, core, T, topo):
         inc(v.tensor_scalar(T.cntI[:, 3 - j::8], T.wi[:, 0:64], 5 * j, 31, ALU.arith_shift_right, ALU.bitwise_and), "dg")
         inc(v.tensor_scalar(T.cntI[:, 4 + j::8], T.wi[:, 64:128], 5 * j, 31, ALU.arith_shift_right, ALU.bitwise_and), "dg")
     wait(v, "dg")
-    inc(v.tensor_copy(T.cntB[:], T.cntI[:]), "cb")
+    for r in farr + nearr:
+        inc(v.tensor_copy(T.cntB[:, r * 64:r * 64 + 64], T.cntI[:, r * 64:r * 64 + 64]), "cb" if r in farr else "cbn")
     inc(v.tensor_copy(T.landC[:, me * 64:me * 64 + 64], T.cntI[:, me * 64:me * 64 + 64]), "cbo")
     wait(g, "cb")
-    spread(lambda r: T.cntB[:, r * 64:r * 64 + 64], T.landC[:, me * 64:me * 64 + 64], T.relC[:], "aC", "hC", "lsC")
+    spread(lambda r: T.cntB[:, r * 64:r * 64 + 64], T.landC[:, me * 64:me * 64 + 64], T.relC[:], "aC", "hC", "lsC", "cbn")
     wait(v, "c4")
     inc(v.tensor_scalar(T.mt[:], T.irr[:], T.cf[:, 0:1], None, ALU.is_gt), "c5")
     inc(v.tensor_scalar(T.c99[:], T.irc[:], -99.0, None, ALU.add), "c5")
-    inc(v.memset(T.cur[:], 0.0), "ms")
-    wait(pe, "c4")
-    for new in ([(2, 6, R[1])], [(3, 6, R[2]), (5, 2, T.Ib[:])], [(4, 6, R[3])]):
-        if new[0][0] != 2:
-            wait(pe, "chv")
-        for t, a, b in new:
-            inc(pe.matmul(T.p1[:, 128 * t - 256:128 * t - 128], R[a], b, True, True), "chp")
-        wait(v, "chp")
-        for t, a, b in new:
-            inc(v.tensor_copy(R[t], T.p1[:, 128 * t - 256:128 * t - 128]), "chv")
-    wait(v, "c5")
-    inc(v.tensor_tensor(T.tb[:], T.mt[:], T.c99[:], ALU.mult), "c6")
     for r in range(NDMA, 8):
         inc(v.tensor_scalar(T.Sel[:, r * 128:r * 128 + 128], T.ir16[:], T.cf[:, 3:4], T.rm[:, r:r + 1], ALU.is_equal, ALU.mult), "c7")
     inc(v.memset(T.zf[:], 0.0), "ms")
     inc(v.memset(T.base[:, 0:1], 0.0), "ms")
-    inc(v.memset(T.cO[:, 256:288], 0.0), "ms")
+    inc(v.memset(T.zc[:], 0.0), "ms")
     inc(v.memset(T.T1[:, NB:NB + 16], 0.0), "ms")
+    wait(v, "c5")
+    inc(v.tensor_tensor(T.tb[:], T.mt[:], T.c99[:], ALU.mult), "c6")
     wait(v, "c6")
     inc(v.tensor_scalar(T.TB[:], T.tb[:], 99.0, None, ALU.add), "c7")
 
@@ -229,126 +215,74 @@ def rank_program(g, core, T, topo):
     inc(sy.dma_start(T.PSl[:, 0:128], T.landP[:]), "psl", 16)
     inc(sy.dma_start(T.PSl[:, 128:160], T.landS[:]), "psl", 16)
     wait(v, "psl", "ms")
+    inc(v.tensor_copy(T.CWu[:], T.PSl[:, 0:128]), "cu")
     inc(v.tensor_copy(T.patb[:], T.PSl[:, 0:128]), "cu")
     inc(v.tensor_scalar(T.w8[:], T.PSl[:, 128:160], 8.0, None, ALU.mult), "w8")
-    wait(pe, "cu", "chv")
-    for t in range(8):
-        inc(pe.matmul(T.p0[:, 16 * t:16 * t + 16], R[t], T.patb[:, 16 * t:16 * t + 16], True, True), "pt")
-    wait(v, "pt", "w8")
-    inc(v.tensor_copy(T.CWu[:], T.p0[:, 0:128]), "cwu")
-    for t in range(8):
-        inc(v.tensor_copy(T.cur[:, 32 * t:32 * t + 16], T.p0[:, 16 * t:16 * t + 16]), "cwp")
-    wait(v, "cwp")
-    inc(v.transpose(T.cO[:, 0:256], T.cur[:]), "cw")
+    wait(v, "cu", "w8")
     for h in range(2):
-        inc(v.tensor_tensor(T["W%d" % h][:, 0:16], T.w8[:, 16 * h:16 * h + 16], T.cur[:, 0:16], ALU.add), "wini")
+        inc(v.tensor_tensor(T["W%d" % h][:], T.w8[:, 16 * h:16 * h + 16], T.patb[:, 0:16], ALU.add), "wini")
 
     def rows(t):
-        inc(s.activation(T.CM[:, 256 * t:256 * t + 256], T.TC[:, 0:8].indirect(T.CWu[:, 16 * t:16 * t + 16]), ACT.Copy), "cm")
-    wait(s, "cwu", "c4")
+        lst = T.CWo[:, 8 * t - 8:8 * t + 8] if t % 2 else T.CWu[:, 16 * t:16 * t + 16]
+        inc(s.activation(T.CM[:, 256 * t:256 * t + 256], T.TC[:, 0:8].indirect(lst), ACT.Copy), "cm")
+
+    wait(s, "cu", "c4")
+    for i in range(4):
+        inc(s.activation(T.SW[:, 256 * i:256 * i + 256], T.LV[:, 0:8].indirect(T.CWu[:, 32 * i + 16:32 * i + 32]), ACT.Copy), "sw")
     rows(0)
-
-    def t1(q, r, sem):
-        wait(q, "aL%d" % r)
-        for G in range(8):
-            inc(q.dma_start(T.T1[16 * G:16 * G + 16, r * 1024:(r + 1) * 1024], T.landL[r * 128:(r + 1) * 128, :]), sem, 16)
-    for r in nearr + farr[2:]:
-        t1(sy, r, "t1")
-    for r in farr[:2]:
-        t1(s, r, "t1s")
-
-    wait(pe, "aC", "cbo", "on")
-    for c in range(8):
-        inc(pe.matmul(T.p3[:, c * 64:c * 64 + 64], T.ones[:], T.landC[:, c::8], True, True), "tot")
-    inc(pe.matmul(T.p2[:], T.Tri[:], T.landC[:], True, True), "tri")
-    wait(v, "tot")
-    inc(v.tensor_tensor_scan(T.base[:, 1:513], T.p3[:], T.zf[:], 0.0, ALU.add, ALU.add), "sc")
-    wait(v, "sc", "tri")
-    for c in range(8):
-        inc(v.tensor_tensor(T.HL[:, c * 64:c * 64 + 64], T.p2[:, c::8], T.base[:, c * 64:c * 64 + 64], ALU.add), "hb" if c < 4 else "hb2")
-    inc(v.tensor_copy(T.ehl[:, 0:8], T.base[:, 64:513:64]), "eh")
-    for c in range(8):
-        if c % 4 == 0:
-            wait(pe, "hb2" if c else "hb")
-        inc(pe.matmul(T.p4[:, c * 64:c * 64 + 64], T.Tri[:], T.landC[:, c::8], True, False), "ml")
-        inc(pe.matmul(T.p4[:, c * 64:c * 64 + 64], T.nI[:], T.HL[:, c * 64:c * 64 + 64], False, True), "ml")
-    wait(v, "eh")
-    inc(v.tensor_tensor(T.ehl[:, 8:16], T.base[:, 64:513:64], T.ehl[:, 0:8], ALU.subtract), "el")
-    wait(v, "ml")
-    inc(v.tensor_tensor(T.HL[:, 512:1024], T.p4[:], T.base[:, 0:512], ALU.add), "lo")
-    wait(v, "el")
-    inc(v.tensor_tensor(T.et[:], T.ehl[:], T.m16[:], ALU.mult), "et")
-    wait(pe, "lo", "es", "ev")
-    for j in range(8):
-        inc(pe.transpose((T.pA if j < 4 else T.pB)[:, j % 4 * 128:j % 4 * 128 + 128], T.HL[:, j::8], T.Ib[:]), "tS" if j < 4 else "tS2")
-    wait(v, "tS")
-    inc(v.tensor_copy(T.S2[:, 0:512], T.pA[:, 0:512]), "s2v")
-    wait(s, "tS2")
-    inc(s.activation(T.S2[:, 512:1024], T.pB[:, 0:512], ACT.Copy), "s2s")
-    wait(v, "et")
-    inc(v.tensor_reduce(T.e1[:], T.et[:], AxisListType.X, ALU.add), "e1")
-    wait(sy, "s2v", "s2s")
-    for r in range(NDMA):
-        for G in range(8):
-            inc(sy.dma_start(T.T2[16 * G:16 * G + 16, r * 1024:(r + 1) * 1024], T.S2[r::8, :]), "t2", 16)
-    wait(pe, "s2v", "c7")
-    i = 0
-    for hf in range(2):
-        if hf:
-            wait(pe, "s2s")
-        for r in range(NDMA, 8):
-            k = i % 4
-            if i >= 4:
-                wait(pe, "rb%d" % k)
-            inc(pe.matmul(T["p%d" % k][:], T.Sel[:, r * 128:r * 128 + 128], T.S2[:, 512 * hf:512 * hf + 512], True, True), "rp%d" % k)
-            o = T.T2[:, r * 1024 + 512 * hf:r * 1024 + 512 * hf + 512]
-            if i % 2 == 0:
-                wait(v, "rp%d" % k)
-                inc(v.tensor_copy(o, T["p%d" % k][:]), "rb%d" % k)
-            else:
-                wait(s, "rp%d" % k)
-                inc(s.activation(o, T["p%d" % k][:], ACT.Copy), "rb%d" % k)
-            i += 1
-    wait(v, "e1")
-    inc(v.tensor_copy(T.T2[:, NB:NB + 1], T.e1[:]), "end")
+    wait(pe, "sw", "c4")
+    for i in range(4):
+        for x in range(2):
+            inc(pe.matmul(T.p5[:, 16 * i + 8 * x:16 * i + 8 * x + 8], T.SW[:, 256 * i + 128 * x:256 * i + 128 * x + 128],
+                          T.Ind1[:], True, True), "swp")
+    wait(v, "swp")
+    inc(v.tensor_copy(T.CWo[:], T.p5[:, 0:64]), "cwo")
+    inc(v.tensor_copy(T.cOo[:], T.p5[:, 0:64]), "cwo")
+    wait(v, "cwo")
+    wait(s, "cwo")
 
     O = [T.p4, T.p5]
 
-    def small1(h, t):
-        W = T["W%d" % h]
-        if t > 0:
-            wait(v, "pO%d" % h)
-            inc(v.transpose(W[:, 0:32], O[h][:, 0:32]), "vT%d" % h)
-            wait(v, "vT%d" % h)
-        else:
+    def state(h, t):
+        if t == 0:
+            W = T["W%d" % h][:]
             wait(v, "wini")
+        else:
+            W = O[h][:, 0:16]
+            wait(v, "pO%d" % h)
         if t == 8:
-            inc(v.tensor_scalar(T.Res[:, 16 * h:16 * h + 16], W[:, 0:16], 0.125, None, ALU.mult), "rs")
+            inc(v.tensor_scalar(T.Res[:, 16 * h:16 * h + 16], W, 0.125, None, ALU.mult), "rs")
             return
-        inc(v.tensor_copy(T["qi%d" % h][:], W[:, 0:16]), "vC%d" % h)
-        inc(v.tensor_scalar(T["la%d" % h][:], W[:, 0:16], 1.0 / 128, -(0.5 - 1.0 / 256), ALU.mult, ALU.add), "vL%d" % h)
+        inc(v.tensor_scalar(T["la%d" % h][:], W, 1.0 / 128, -(0.5 - 1.0 / 256), ALU.mult, ALU.add), "vL%d" % h)
+        inc(v.tensor_copy(T["qi%d" % h][:], W), "vC%d" % h)
+        if t > 0:
+            letters_at(h, t)
 
-    def small2(h, t):
-        if t == 8:
-            return
-        wait(v, "vC%d" % h)
-        inc(v.tensor_scalar(T["rr%d" % h][:], T["qi%d" % h][:], 127, None, ALU.bitwise_and), "vA%d" % h)
-        wait(v, "vA%d" % h)
-        inc(v.tensor_copy(T["lb%d" % h][:], T["rr%d" % h][:]), "vU%d" % h)
-        wait(s, "vU%d" % h)
+    def letters_at(h, t):
+        wait(s, "vL%d" % h)
         if t == 0 and h == 0:
-            wait(s, "c7")
-        inc(s.activation(T["G%d" % h][:], T.TB[:].indirect(T["lb%d" % h][:]), ACT.Copy), "sG%d" % h)
+            wait(s, "own", "t1", "ms")
+        inc(s.activation(T["L%d" % h][:], T.T1[:, 0:NB + 1].indirect(T["la%d" % h][:]), ACT.Copy), "sG%d" % h)
         if h == 1 and t < 7:
             rows(t + 1)
 
+    def rem(h, t):
+        if t < 8:
+            wait(v, "vC%d" % h)
+            inc(v.tensor_scalar(T["rr%d" % h][:], T["qi%d" % h][:], 127, None, ALU.bitwise_and), "vA%d" % h)
+
+    def rem16(h, t):
+        if t < 8:
+            wait(v, "vA%d" % h)
+            inc(v.tensor_copy(T["lb%d" % h][:], T["rr%d" % h][:]), "vU%d" % h)
+
     def letters(h, t, first):
-        inc(pe.matmul(O[h][:, 0:32], T.Ih[:], T.cO[:, 32 * t + 32:32 * t + 64], first, not first), "pO%d" % h)
+        nxt = T.zc[:] if t == 7 else T.cOo[:, 8 * t:8 * t + 16] if t % 2 == 0 else T.patb[:, 16 * t + 16:16 * t + 32]
+        inc(pe.matmul(O[h][:, 0:16], T.Ih[:], nxt, first, not first), "pO%d" % h)
 
     def sums(h, X):
-        for A in range(4):
-            for ch in range(4):
-                inc(pe.matmul(O[h][32 * A:32 * A + 16, 8 * ch:8 * ch + 8], X[:, 4 * A + ch::16], T.Ind8[:], False, False), "pO%d" % h)
+        for x in range(2):
+            inc(pe.matmul(O[h][:, 8 * x:8 * x + 8], X[:, 128 * x:128 * x + 128], T.Ind8[:], False, False), "pO%d" % h)
 
     def occ(h, t):
         if t == 8:
@@ -356,52 +290,131 @@ def rank_program(g, core, T, topo):
         wait(v, "vL%d" % h)
         if h == 0:
             wait(v, "cm")
-        if t == 0 and h == 0:
-            wait(v, "t2", "end", "rb0", "rb1", "rb2", "rb3")
         inc(v.tensor_tensor(T["F%d" % h][:], T.T2[:, 0:NB + 1].indirect(T["la%d" % h][:]), T.CM[:, 256 * t:256 * t + 256], ALU.mult), "vF%d" % h)
         wait(pe, "vF%d" % h)
-        if t == 0 and h == 0:
-            wait(pe, "cw", "ms")
-        letters(h, t, True)
+        if t > 0:
+            letters(h, t, True)
         sums(h, T["F%d" % h])
+        if t == 0:
+            letters(h, t, False)
 
     def fine(h, t):
-        wait(v, "sG%d" % h)
-        if t == 0 and h == 0:
-            wait(v, "own", "t1", "t1s", "ms")
-        inc(v.tensor_tensor(T["E%d" % h][:], T.T1[:, 0:NB + 1].indirect(T["la%d" % h][:]), T["G%d" % h][:], ALU.is_equal), "vE%d" % h)
+        wait(v, "vU%d" % h, "sG%d" % h)
+        inc(v.tensor_tensor(T["E%d" % h][:], T.TB[:].indirect(T["lb%d" % h][:]), T["L%d" % h][:], ALU.is_equal), "vE%d" % h)
         wait(pe, "vE%d" % h)
+        if t == 0:
+            letters(h, t, True)
         sums(h, T["E%d" % h])
-        letters(h, t, False)
+        if t > 0:
+            letters(h, t, False)
 
-    small1(0, 0)
-    small2(0, 0)
+    wait(v, "c7")
+    for h in range(2):
+        state(h, 0)
+    for h in range(2):
+        rem(h, 0)
+    for h in range(2):
+        rem16(h, 0)
+
+    for r in nearr + farr:
+        wait(sy, "aL%d" % r)
+        for G in range(8):
+            inc(sy.dma_start(T.T1[16 * G:16 * G + 16, r * 1024:(r + 1) * 1024], T.landL[r * 128:(r + 1) * 128, :]), "t1", 16)
+
+    wait(pe, "aC", "cbo", "on", "c4")
+    for c in range(8):
+        inc(pe.matmul(T.p3[:, c * 64:c * 64 + 64], T.ones[:], T.landC[:, c::8], True, True), "tot")
+    inc(pe.matmul(T.p2[:], T.Tri[:], T.landC[:], True, True), "tri")
+    wait(v, "tot")
+    inc(v.tensor_tensor_scan(T.base[:, 1:513], T.p3[:], T.zf[:], 0.0, ALU.add, ALU.add), "sc")
+    wait(v, "sc", "tri")
+    for c in range(8):
+        inc(v.tensor_tensor(O[c // 4][:, c % 4 * 64:c % 4 * 64 + 64], T.p2[:, c::8], T.base[:, c * 64:c * 64 + 64], ALU.add),
+            "va%d" % (c // 4))
+    inc(v.tensor_copy(T.ehl[:, 0:8], T.base[:, 64:513:64]), "eh")
+    for k in range(2):
+        wait(s, "va%d" % k)
+        inc(s.activation(T.HL[:, 256 * k:256 * k + 256], O[k][:, 0:256], ACT.Copy), "hi%d" % k)
+        wait(v, "hi%d" % k)
+        inc(v.tensor_tensor(T.HL[:, 512 + 256 * k:768 + 256 * k], O[k][:, 0:256], T.HL[:, 256 * k:256 * k + 256], ALU.subtract), "lo%d" % k)
+    wait(pe, "hi0", "lo0", "hi1", "lo1", "ev")
+    for j in range(8):
+        inc(pe.transpose((T.pA if j < 4 else T.pB)[:, j % 4 * 128:j % 4 * 128 + 128], T.HL[:, j::8], T.Ib[:]), "tS" if j < 4 else "tS2")
+    wait(v, "eh")
+    inc(v.tensor_tensor(T.ehl[:, 8:16], T.base[:, 64:513:64], T.ehl[:, 0:8], ALU.subtract), "el")
+    wait(v, "tS")
+    inc(v.tensor_copy(T.S2[:, 0:512], T.pA[:, 0:512]), "s2a")
+    wait(v, "tS2")
+    inc(v.tensor_copy(T.S2[:, 512:1024], T.pB[:, 0:512]), "s2b")
+    wait(v, "el")
+    inc(v.tensor_tensor(T.et[:], T.ehl[:], T.m16[:], ALU.mult), "et")
+    wait(sy, "s2a", "s2b")
+    for r in range(NDMA):
+        for G in range(8):
+            inc(sy.dma_start(T.T2[16 * G:16 * G + 16, r * 1024:(r + 1) * 1024], T.S2[r::8, :]), "t2", 16)
+
+    wait(pe, "s2a", "c7")
+    pieces = [(r, hf) for hf in range(2) for r in range(NDMA, 8)]
+    for n, (r, hf) in enumerate(pieces):
+        k = n % 4
+        if n == 8 - NDMA:
+            wait(pe, "s2b")
+        if n >= 4:
+            wait(pe, "rb%d" % k)
+        inc(pe.matmul(T["p%d" % k][:], T.Sel[:, r * 128:r * 128 + 128], T.S2[:, 512 * hf:512 * hf + 512], True, True), "rp%d" % k)
+        o = T.T2[:, r * 1024 + 512 * hf:r * 1024 + 512 * hf + 512]
+        q = (v, s)[n % 2]
+        wait(q, "rp%d" % k)
+        inc(v.tensor_copy(o, T["p%d" % k][:]) if q is v else s.activation(o, T["p%d" % k][:], ACT.Copy), "rb%d" % k)
+        left = len(pieces) - 1 - n
+        if left == 4:
+            letters_at(0, 0)
+        if left == 2:
+            letters_at(1, 0)
+            wait(pe, "ms")
+            fine(0, 0)
+        if left == 0:
+            fine(1, 0)
+    wait(v, "et")
+    inc(v.tensor_reduce(T.e1[:], T.et[:], AxisListType.X, ALU.add), "e1")
+    wait(v, "e1")
+    inc(v.tensor_copy(T.T2[:, NB:NB + 1], T.e1[:]), "end")
+    wait(v, "t2", "end", "rb0", "rb1", "rb2", "rb3")
+
     occ(0, 0)
-    small1(1, 0)
-    for t in range(8):
+    occ(1, 0)
+    state(0, 1)
+    rem(0, 1)
+    occ(0, 1)
+    rem16(0, 1)
+    state(1, 1)
+    for t in range(1, 8):
         fine(0, t)
-        small2(1, t)
+        rem(1, t)
         occ(1, t)
-        small1(0, t + 1)
+        rem16(1, t)
+        state(0, t + 1)
         fine(1, t)
-        small2(0, t + 1)
+        rem(0, t + 1)
         occ(0, t + 1)
-        small1(1, t + 1)
+        rem16(0, t + 1)
+        state(1, t + 1)
 
     wait(g, "rs")
     spread(lambda r: T.Res[:], T.landR[:, me * 32:me * 32 + 32], T.relR[:], "aRn", "hR", "lsR")
+    own = slice(16 * me, 16 * me + 16)
 
     def y(q, r, src, sem):
         inc(q.dma_start(T.y[16 * r:16 * r + 16, :], src), sem, 16)
     wait(sy, "rs")
-    y(sy, me, T.Res[me::8, :], "yo")
+    y(sy, me, T.Res[own, :], "yo")
     wait(sy, "aRn")
     for r in nearr:
-        y(sy, r, T.landR[me::8, r * 32:r * 32 + 32], "yo")
+        y(sy, r, T.landR[own, r * 32:r * 32 + 32], "yo")
     wait(sy, "aRf")
     wait(s, "aRf")
     for k, r in enumerate(farr):
-        y((sy, s)[k % 2], r, T.landR[me::8, r * 32:r * 32 + 32], ("yo", "ys")[k % 2])
+        y((sy, s)[k % 2], r, T.landR[own, r * 32:r * 32 + 32], ("yo", "ys")[k % 2])
     wait(sy, "yo")
     wait(s, "ys")
     for name in cnt:

import math
from concourse.bass import DstId, RemoteDMATransfer
from concourse.mybir import dt, AluOpType, AxisListType, ActivationFunctionType

ALU = AluOpType
ACT = ActivationFunctionType
NB = 8192
NDMA = 3


def _sb(dtype, **kw):
    return {n: ("sbuf", [128] + (list(w) if isinstance(w, tuple) else [w]), dtype) for n, w in kw.items()}


SCRATCH = {"sendL": ("dram", [1024, 128], "bfloat16"), "landL": ("dram", [1024, 128], "bfloat16"),
           "relL": ("dram", [128, 128], "bfloat16"),
           "pA": ("psum", [128, 1024], "bfloat16"), "pB": ("psum", [128, 1024], "bfloat16")}
for _n, _w in (("P", 16), ("S", 4)):
    SCRATCH.update({"send" + _n: ("dram", [1024, _w], "int32"), "land" + _n: ("dram", [1024, _w], "int32"),
                    "rel" + _n: ("dram", [128, _w], "int32")})
SCRATCH.update({"p%d" % _k: ("psum", [128, 512], "float32") for _k in range(6)})
SCRATCH.update(_sb("int32", X=(8, 8, 16), wi=128, cntI=512, PSl=160, ip=1, irow=128, ci=8, ir16=128, irc=128, irr=128,
                   qi0=16, qi1=16, rr0=16, rr1=16))
SCRATCH.update(_sb("uint16", CWu=128, CWo=64, la0=16, la1=16, lb0=16, lb1=16))
SCRATCH.update(_sb("float32", landR=256, w8=32, base=516, zf=512, et=16, e1=1, Res=32, cf=8, irf=128, mt=128, c99=128, tb=128,
                   rm=8, m16=16, relR=32, W0=16, W1=16))
SCRATCH.update(_sb("bfloat16", Xb=(8, 128), Ls=1024, clo=1024, chi=1024, cntB=512, landC=512, zc=16, cOo=64, CM=2048, HL=1024,
                   S2=1024, ehl=16, T1=NB + 16, T2=NB + 16, TB=128, TC=8, LV=8, ones=128, Ib=128, Ih=128, Tri=128, SW=1024,
                   Ind1=8, Ind8=8, Sel=1024, patb=128, relC=64, L0=256, L1=256, E0=256, E1=256, F0=256, F1=256))

SEMAPHORES = (["io", "c1", "c2", "c3", "c4", "c5", "c6", "c7", "on", "ms", "xb", "tA", "tB", "ev", "ex0", "ex1", "pc",
               "wi", "dg", "cb", "cbn", "cbo", "spP", "spS", "own2", "stL", "own", "psl", "cu", "sw", "swp", "cwo",
               "w8", "wini", "cm", "tot", "tri", "sc", "va0", "va1", "hi0", "hi1", "lo0", "lo1", "tS", "tS2", "s2a", "s2b", "t2",
               "t1", "eh", "el", "et", "e1", "end", "rs", "yo", "ys", "lsP", "lsS", "lsL", "lsC", "lsR", "aP", "aS", "aC",
               "aRn", "aRf", "hP", "hS", "hL", "hC", "hR", "hl"]
              + ["ld%d" % k for k in range(4)] + ["aL%d" % k for k in range(8)]
              + ["rp%d" % k for k in range(4)] + ["rb%d" % k for k in range(4)]
              + ["%s%d" % (n, h) for n in ("vC", "vL", "vA", "vU", "sG", "vF", "vE", "pO") for h in range(2)])
WN, WF = 2, 4


def routes(c, T, topo):
    near = [d for d in T.cores if d != c and topo.may_write(c, d)]
    far = [d for d in T.cores if d != c and not topo.may_write(c, d)]
    via = []
    for k, d in enumerate(far):
        hs = [h for h in topo.cores_of(c) if h != c and topo.may_write(h, d)]
        via.append((d, hs[k % len(hs)]))
    return near, via


def hand_on(g, core, T, topo):
    for c in T.cores:
        if core not in topo.cores_of(c):
            continue
        for d, h in routes(c, T, topo)[1]:
            if h != core:
                continue
            r = T.rank_of(c)
            rid, pid = topo.addr(d, core)
            m = topo.mask(core, d)
            n = len(topo.engines(core, d))
            jobs = [("hP", T.relP[:], T.landP[r * 128:(r + 1) * 128, :], "aP"),
                    ("hS", T.relS[:], T.landS[r * 128:(r + 1) * 128, :], "aS"),
                    ("hL", T.relL[:], T.landL[r * 128:(r + 1) * 128, :], "aL%d" % r),
                    ("hC", T.relC[:], T.landC[:, r * 64:(r + 1) * 64], "aC"),
                    ("hR", T.relR[:], T.landR[:, r * 32:(r + 1) * 32], "aRf")]
            for hs, src, dst, a in jobs:
                g.wait_ge(T.sem[hs], WF)
                g.remote_dma(out_ap=dst, in_ap=src, remote_sem=T.sem[a], local_sem=T.sem.hl, pid=pid, routing_id=rid, dma_engine_mask=m)
            g.wait_ge(T.sem.hl, n * len(jobs))


def rank_program(g, core, T, topo):
    me = T.rank_of(core)
    if me is None:
        hand_on(g, core, T, topo)
        return
    v, s, pe, sy = g.vector, g.scalar, g.tensor, g.sync
    near, via = routes(core, T, topo)
    nearr = [T.rank_of(d) for d in near]
    farr = [T.rank_of(d) for d, h in via]
    nfar = {T.rank_of(c): len(topo.engines(h, core)) for c in T.cores if c != core for d, h in routes(c, T, topo)[1] if d == core}
    off = topo.engines(core, near[0])
    onc = topo.engines(core, via[0][1])
    cnt, seen = {}, {}

    def inc(ins, name, n=1):
        ins.then_inc(T.sem[name], n)
        cnt[name] = cnt.get(name, 0) + n

    def wait(q, *names):
        for name in names:
            q.wait_ge(T.sem[name], cnt[name])
            seen[name] = max(seen.get(name, 0), cnt[name])

    def fan(jobs, engines, w, srcs, out, sem, lsem):
        tr = []
        for k, (d, to) in enumerate(jobs):
            rid, pid = topo.addr(to, core)
            tr.append(RemoteDMATransfer(dst_ids=[DstId(rid=rid, pnc=pid)], dma_engine_mask=sum(1 << e for e in engines[w * k:w * k + w]),
                                        remote_sem=T.sem[sem], src=srcs(T.rank_of(d)), dst=out))
        g.remote_dma_fused(tr, local_sem=T.sem[lsem])
        cnt[lsem] = cnt.get(lsem, 0) + w * len(tr)

    def spread(srcs, dst, rel, arr, hsem, lsem, between=None):
        fan(via, onc, WF, srcs, rel, hsem, lsem)
        if between:
            wait(g, between)
        fan([(d, d) for d in near], off, WN, srcs, dst, arr, lsem)

    cnt["aP"] = cnt["aS"] = cnt["aC"] = WN * len(near) + sum(nfar.values())
    cnt["aRn"] = WN * len(near)
    cnt["aRf"] = sum(nfar.values())
    for r in nearr:
        cnt["aL%d" % r] = WN
    for r in farr:
        cnt["aL%d" % r] = nfar[r]
    mine = slice(me * 128, me * 128 + 128)

    inc(g.iota(T.ip[:], [[0, 1]], 0, 1), "io")
    inc(g.iota(T.irow[:], [[1, 128]], 0, 0), "io")
    inc(sy.dma_start(T.sendP[:], T.pats[:]), "spP", 16)
    inc(s.dma_start(T.sendS[:], T.starts[:]), "spS", 16)
    for q in range(8):
        inc((sy if q % 2 == 0 else s).dma_start(T.X[:, q], T.bwt[q]), "ld%d" % (q // 2), 16)
    inc(sy.dma_start(T.landP[mine, :], T.pats[16 * me:16 * me + 16, :]), "own2", 16)
    inc(s.dma_start(T.landS[mine, :], T.starts[16 * me:16 * me + 16, :]), "own2", 16)
    wait(g, "spP")
    spread(lambda r: T.sendP[r * 128:(r + 1) * 128, :], T.landP[mine, :], T.relP[:], "aP", "hP", "lsP")
    wait(g, "spS")
    spread(lambda r: T.sendS[r * 128:(r + 1) * 128, :], T.landS[mine, :], T.relS[:], "aS", "hS", "lsS")
    wait(v, "io")
    inc(v.tensor_scalar(T.ci[:, 0:1], T.ip[:], 15, None, ALU.bitwise_and), "c1")
    inc(v.tensor_scalar(T.ci[:, 1:2], T.ip[:], 4, None, ALU.arith_shift_right), "c1")
    inc(v.tensor_scalar(T.ci[:, 2:3], T.ip[:], 7, None, ALU.bitwise_and), "c1")
    inc(v.tensor_scalar(T.ci[:, 3:4], T.ip[:], 3, None, ALU.arith_shift_right), "c1")
    inc(v.tensor_copy(T.cf[:, 4:5], T.ip[:]), "c1")
    inc(v.tensor_copy(T.irf[:], T.irow[:]), "c1")
    wait(v, "c1")
    inc(v.tensor_copy(T.cf[:, 0:4], T.ci[:, 0:4]), "c2")
    inc(v.tensor_scalar(T.Ib[:], T.irow[:], T.cf[:, 4:5], None, ALU.is_equal), "c2")
    wait(v, "c2")
    inc(v.tensor_scalar(T.Ind1[:], T.irow[:, 0:8], T.cf[:, 1:2], None, ALU.is_equal), "c3")
    wait(s, "c1")
    inc(s.activation(T.ones[:], T.irf[:], ACT.Exp, scale=0.0), "on")

    for q in range(8):
        if q % 2 == 0:
            wait(v, "ld%d" % (q // 2))
        inc(v.tensor_copy(T.Xb[:, :, 16 * q:16 * q + 16], T.X[:, q]), "xb")
    wait(pe, "xb", "c2")
    for u in range(8):
        inc(pe.transpose((T.pA if u < 4 else T.pB)[:, u % 4 * 128:u % 4 * 128 + 128], T.Xb[:, u, :], T.Ib[:]), "tA" if u < 4 else "tB")
    for u in range(8):
        if u % 4 == 0:
            wait(v, "tB" if u else "tA")
        inc(v.tensor_copy(T.Ls[:, u::8], (T.pA if u < 4 else T.pB)[:, u % 4 * 128:u % 4 * 128 + 128]), "ev")
    wait(sy, "ev")
    inc(sy.dma_start(T.sendL[:], T.Ls[:]), "stL", 16)
    for G in range(8):
        inc(sy.dma_start(T.T1[16 * G:16 * G + 16, me * 1024:(me + 1) * 1024], T.Ls[16 * me:16 * me + 16, :]), "own", 16)
    wait(g, "stL")
    spread(lambda r: T.sendL[r * 128:(r + 1) * 128, :], T.landL[mine, :], T.relL[:], "aL%d" % me, "hL", "lsL")

    wait(s, "ev")
    k32 = math.log(32.0)
    for h in range(2):
        a, b = 512 * h, 512 * h + 512
        inc(s.activation(T.clo[:, a:b], T.Ls[:, a:b], ACT.Exp, bias=3 * k32, scale=-k32), "ex%d" % h)
        inc(s.activation(T.chi[:, a:b], T.Ls[:, a:b], ACT.Exp, bias=-4 * k32, scale=k32), "ex%d" % h)
    wait(pe, "c3")
    for h in range(2):
        wait(pe, "ex%d" % h)
        for w, code in enumerate((T.clo, T.chi)):
            for j in range(4 * h, 4 * h + 4):
                inc(pe.matmul(T.p0[:, w * 64 + j:w * 64 + 64:8], code[:, j * 128:j * 128 + 128], T.Ind1[:], True, True), "pc")
    inc(v.tensor_scalar(T.ir16[:], T.irow[:], 15, None, ALU.bitwise_and), "c4")
    inc(v.tensor_scalar(T.irc[:], T.irow[:], 7, None, ALU.bitwise_and), "c4")
    inc(v.tensor_scalar(T.irr[:], T.irow[:], 3, None, ALU.arith_shift_right), "c4")
    inc(v.tensor_scalar(T.Tri[:], T.irow[:], T.cf[:, 4:5], None, ALU.is_gt), "c4")
    inc(v.tensor_scalar(T.Ih[:], T.irow[:], T.cf[:, 4:5], 0.5, ALU.is_equal, ALU.mult), "c4")
    inc(v.tensor_scalar(T.Ind8[:], T.irow[:, 0:8], T.cf[:, 1:2], 8.0, ALU.is_equal, ALU.mult), "c4")
    inc(v.tensor_scalar(T.TC[:], T.irow[:, 0:8], T.cf[:, 2:3], None, ALU.is_equal), "c4")
    inc(v.tensor_scalar(T.LV[:], T.irow[:, 0:8], 1.0 / 16, None, ALU.mult), "c4")
    inc(v.tensor_scalar(T.rm[:], T.irow[:, 0:8], T.cf[:, 2:3], None, ALU.is_equal), "c4")
    inc(v.tensor_scalar(T.m16[:], T.irow[:, 0:16], T.cf[:, 0:1], None, ALU.is_equal), "c4")
    wait(v, "pc")
    inc(v.tensor_scalar(T.wi[:], T.p0[:, 0:128], -0.25, None, ALU.add), "wi")
    wait(v, "wi")
    for j in range(4):
        inc(v.tensor_scalar(T.cntI[:, 3 - j::8], T.wi[:, 0:64], 5 * j, 31, ALU.arith_shift_right, ALU.bitwise_and), "dg")
        inc(v.tensor_scalar(T.cntI[:, 4 + j::8], T.wi[:, 64:128], 5 * j, 31, ALU.arith_shift_right, ALU.bitwise_and), "dg")
    wait(v, "dg")
    for r in farr + nearr:
        inc(v.tensor_copy(T.cntB[:, r * 64:r * 64 + 64], T.cntI[:, r * 64:r * 64 + 64]), "cb" if r in farr else "cbn")
    inc(v.tensor_copy(T.landC[:, me * 64:me * 64 + 64], T.cntI[:, me * 64:me * 64 + 64]), "cbo")
    wait(g, "cb")
    spread(lambda r: T.cntB[:, r * 64:r * 64 + 64], T.landC[:, me * 64:me * 64 + 64], T.relC[:], "aC", "hC", "lsC", "cbn")
    wait(v, "c4")
    inc(v.tensor_scalar(T.mt[:], T.irr[:], T.cf[:, 0:1], None, ALU.is_gt), "c5")
    inc(v.tensor_scalar(T.c99[:], T.irc[:], -99.0, None, ALU.add), "c5")
    for r in range(NDMA, 8):
        inc(v.tensor_scalar(T.Sel[:, r * 128:r * 128 + 128], T.ir16[:], T.cf[:, 3:4], T.rm[:, r:r + 1], ALU.is_equal, ALU.mult), "c7")
    inc(v.memset(T.zf[:], 0.0), "ms")
    inc(v.memset(T.base[:, 0:1], 0.0), "ms")
    inc(v.memset(T.zc[:], 0.0), "ms")
    inc(v.memset(T.T1[:, NB:NB + 16], 0.0), "ms")
    wait(v, "c5")
    inc(v.tensor_tensor(T.tb[:], T.mt[:], T.c99[:], ALU.mult), "c6")
    wait(v, "c6")
    inc(v.tensor_scalar(T.TB[:], T.tb[:], 99.0, None, ALU.add), "c7")

    wait(sy, "aP", "aS", "own2")
    inc(sy.dma_start(T.PSl[:, 0:128], T.landP[:]), "psl", 16)
    inc(sy.dma_start(T.PSl[:, 128:160], T.landS[:]), "psl", 16)
    wait(v, "psl", "ms")
    inc(v.tensor_copy(T.CWu[:], T.PSl[:, 0:128]), "cu")
    inc(v.tensor_copy(T.patb[:], T.PSl[:, 0:128]), "cu")
    inc(v.tensor_scalar(T.w8[:], T.PSl[:, 128:160], 8.0, None, ALU.mult), "w8")
    wait(v, "cu", "w8")
    for h in range(2):
        inc(v.tensor_tensor(T["W%d" % h][:], T.w8[:, 16 * h:16 * h + 16], T.patb[:, 0:16], ALU.add), "wini")

    def rows(t):
        lst = T.CWo[:, 8 * t - 8:8 * t + 8] if t % 2 else T.CWu[:, 16 * t:16 * t + 16]
        inc(s.activation(T.CM[:, 256 * t:256 * t + 256], T.TC[:, 0:8].indirect(lst), ACT.Copy), "cm")

    wait(s, "cu", "c4")
    for i in range(4):
        inc(s.activation(T.SW[:, 256 * i:256 * i + 256], T.LV[:, 0:8].indirect(T.CWu[:, 32 * i + 16:32 * i + 32]), ACT.Copy), "sw")
    rows(0)
    wait(pe, "sw", "c4")
    for i in range(4):
        for x in range(2):
            inc(pe.matmul(T.p5[:, 16 * i + 8 * x:16 * i + 8 * x + 8], T.SW[:, 256 * i + 128 * x:256 * i + 128 * x + 128],
                          T.Ind1[:], True, True), "swp")
    wait(v, "swp")
    inc(v.tensor_copy(T.CWo[:], T.p5[:, 0:64]), "cwo")
    inc(v.tensor_copy(T.cOo[:], T.p5[:, 0:64]), "cwo")
    wait(v, "cwo")
    wait(s, "cwo")

    O = [T.p4, T.p5]

    def state(h, t):
        if t == 0:
            W = T["W%d" % h][:]
            wait(v, "wini")
        else:
            W = O[h][:, 0:16]
            wait(v, "pO%d" % h)
        if t == 8:
            inc(v.tensor_scalar(T.Res[:, 16 * h:16 * h + 16], W, 0.125, None, ALU.mult), "rs")
            return
        inc(v.tensor_scalar(T["la%d" % h][:], W, 1.0 / 128, -(0.5 - 1.0 / 256), ALU.mult, ALU.add), "vL%d" % h)
        inc(v.tensor_copy(T["qi%d" % h][:], W), "vC%d" % h)
        if t > 0:
            letters_at(h, t)

    def letters_at(h, t):
        wait(s, "vL%d" % h)
        if t == 0 and h == 0:
            wait(s, "own", "t1", "ms")
        inc(s.activation(T["L%d" % h][:], T.T1[:, 0:NB + 1].indirect(T["la%d" % h][:]), ACT.Copy), "sG%d" % h)
        if h == 1 and t < 7:
            rows(t + 1)

    def rem(h, t):
        if t < 8:
            wait(v, "vC%d" % h)
            inc(v.tensor_scalar(T["rr%d" % h][:], T["qi%d" % h][:], 127, None, ALU.bitwise_and), "vA%d" % h)

    def rem16(h, t):
        if t < 8:
            wait(v, "vA%d" % h)
            inc(v.tensor_copy(T["lb%d" % h][:], T["rr%d" % h][:]), "vU%d" % h)

    def letters(h, t, first):
        nxt = T.zc[:] if t == 7 else T.cOo[:, 8 * t:8 * t + 16] if t % 2 == 0 else T.patb[:, 16 * t + 16:16 * t + 32]
        inc(pe.matmul(O[h][:, 0:16], T.Ih[:], nxt, first, not first), "pO%d" % h)

    def sums(h, X):
        for x in range(2):
            inc(pe.matmul(O[h][:, 8 * x:8 * x + 8], X[:, 128 * x:128 * x + 128], T.Ind8[:], False, False), "pO%d" % h)

    def occ(h, t):
        if t == 8:
            return
        wait(v, "vL%d" % h)
        if h == 0:
            wait(v, "cm")
        inc(v.tensor_tensor(T["F%d" % h][:], T.T2[:, 0:NB + 1].indirect(T["la%d" % h][:]), T.CM[:, 256 * t:256 * t + 256], ALU.mult), "vF%d" % h)
        wait(pe, "vF%d" % h)
        if t > 0:
            letters(h, t, True)
        sums(h, T["F%d" % h])
        if t == 0:
            letters(h, t, False)

    def fine(h, t):
        wait(v, "vU%d" % h, "sG%d" % h)
        inc(v.tensor_tensor(T["E%d" % h][:], T.TB[:].indirect(T["lb%d" % h][:]), T["L%d" % h][:], ALU.is_equal), "vE%d" % h)
        wait(pe, "vE%d" % h)
        if t == 0:
            letters(h, t, True)
        sums(h, T["E%d" % h])
        if t > 0:
            letters(h, t, False)

    wait(v, "c7")
    for h in range(2):
        state(h, 0)
    for h in range(2):
        rem(h, 0)
    for h in range(2):
        rem16(h, 0)

    for r in nearr + farr:
        wait(sy, "aL%d" % r)
        for G in range(8):
            inc(sy.dma_start(T.T1[16 * G:16 * G + 16, r * 1024:(r + 1) * 1024], T.landL[r * 128:(r + 1) * 128, :]), "t1", 16)

    wait(pe, "aC", "cbo", "on", "c4")
    for c in range(8):
        inc(pe.matmul(T.p3[:, c * 64:c * 64 + 64], T.ones[:], T.landC[:, c::8], True, True), "tot")
    inc(pe.matmul(T.p2[:], T.Tri[:], T.landC[:], True, True), "tri")
    wait(v, "tot")
    inc(v.tensor_tensor_scan(T.base[:, 1:513], T.p3[:], T.zf[:], 0.0, ALU.add, ALU.add), "sc")
    wait(v, "sc", "tri")
    for c in range(8):
        inc(v.tensor_tensor(O[c // 4][:, c % 4 * 64:c % 4 * 64 + 64], T.p2[:, c::8], T.base[:, c * 64:c * 64 + 64], ALU.add),
            "va%d" % (c // 4))
    inc(v.tensor_copy(T.ehl[:, 0:8], T.base[:, 64:513:64]), "eh")
    for k in range(2):
        wait(s, "va%d" % k)
        inc(s.activation(T.HL[:, 256 * k:256 * k + 256], O[k][:, 0:256], ACT.Copy), "hi%d" % k)
        wait(v, "hi%d" % k)
        inc(v.tensor_tensor(T.HL[:, 512 + 256 * k:768 + 256 * k], O[k][:, 0:256], T.HL[:, 256 * k:256 * k + 256], ALU.subtract), "lo%d" % k)
    wait(pe, "hi0", "lo0", "hi1", "lo1", "ev")
    for j in range(8):
        inc(pe.transpose((T.pA if j < 4 else T.pB)[:, j % 4 * 128:j % 4 * 128 + 128], T.HL[:, j::8], T.Ib[:]), "tS" if j < 4 else "tS2")
    wait(v, "eh")
    inc(v.tensor_tensor(T.ehl[:, 8:16], T.base[:, 64:513:64], T.ehl[:, 0:8], ALU.subtract), "el")
    wait(v, "tS")
    inc(v.tensor_copy(T.S2[:, 0:512], T.pA[:, 0:512]), "s2a")
    wait(v, "tS2")
    inc(v.tensor_copy(T.S2[:, 512:1024], T.pB[:, 0:512]), "s2b")
    wait(v, "el")
    inc(v.tensor_tensor(T.et[:], T.ehl[:], T.m16[:], ALU.mult), "et")
    wait(sy, "s2a", "s2b")
    for r in range(NDMA):
        for G in range(8):
            inc(sy.dma_start(T.T2[16 * G:16 * G + 16, r * 1024:(r + 1) * 1024], T.S2[r::8, :]), "t2", 16)

    wait(pe, "s2a", "c7")
    pieces = [(r, hf) for hf in range(2) for r in range(NDMA, 8)]
    for n, (r, hf) in enumerate(pieces):
        k = n % 4
        if n == 8 - NDMA:
            wait(pe, "s2b")
        if n >= 4:
            wait(pe, "rb%d" % k)
        inc(pe.matmul(T["p%d" % k][:], T.Sel[:, r * 128:r * 128 + 128], T.S2[:, 512 * hf:512 * hf + 512], True, True), "rp%d" % k)
        o = T.T2[:, r * 1024 + 512 * hf:r * 1024 + 512 * hf + 512]
        q = (v, s)[n % 2]
        wait(q, "rp%d" % k)
        inc(v.tensor_copy(o, T["p%d" % k][:]) if q is v else s.activation(o, T["p%d" % k][:], ACT.Copy), "rb%d" % k)
        left = len(pieces) - 1 - n
        if left == 4:
            letters_at(0, 0)
        if left == 2:
            letters_at(1, 0)
            wait(pe, "ms")
            fine(0, 0)
        if left == 0:
            fine(1, 0)
    wait(v, "et")
    inc(v.tensor_reduce(T.e1[:], T.et[:], AxisListType.X, ALU.add), "e1")
    wait(v, "e1")
    inc(v.tensor_copy(T.T2[:, NB:NB + 1], T.e1[:]), "end")
    wait(v, "t2", "end", "rb0", "rb1", "rb2", "rb3")

    occ(0, 0)
    occ(1, 0)
    state(0, 1)
    rem(0, 1)
    occ(0, 1)
    rem16(0, 1)
    state(1, 1)
    for t in range(1, 8):
        fine(0, t)
        rem(1, t)
        occ(1, t)
        rem16(1, t)
        state(0, t + 1)
        fine(1, t)
        rem(0, t + 1)
        occ(0, t + 1)
        rem16(0, t + 1)
        state(1, t + 1)

    wait(g, "rs")
    spread(lambda r: T.Res[:], T.landR[:, me * 32:me * 32 + 32], T.relR[:], "aRn", "hR", "lsR")
    own = slice(16 * me, 16 * me + 16)

    def y(q, r, src, sem):
        inc(q.dma_start(T.y[16 * r:16 * r + 16, :], src), sem, 16)
    wait(sy, "rs")
    y(sy, me, T.Res[own, :], "yo")
    wait(sy, "aRn")
    for r in nearr:
        y(sy, r, T.landR[own, r * 32:r * 32 + 32], "yo")
    wait(sy, "aRf")
    wait(s, "aRf")
    for k, r in enumerate(farr):
        y((sy, s)[k % 2], r, T.landR[own, r * 32:r * 32 + 32], ("yo", "ys")[k % 2])
    wait(sy, "yo")
    wait(s, "ys")
    for name in cnt:
        if seen.get(name, 0) < cnt[name]:
            wait(g, name)
